import numpy as np
import ml_dtypes


def mxq(x, axis, fmt="e4m3"):
    dtype, down = {"e4m3": (ml_dtypes.float8_e4m3fn, 7), "e5m2": (ml_dtypes.float8_e5m2, 14)}[fmt]
    v = np.moveaxis(np.asarray(x, np.float32).astype(ml_dtypes.bfloat16).astype(np.float64), axis, -1)
    blocks = v.reshape(v.shape[:-1] + (-1, 32))
    amax = np.abs(blocks).max(-1, keepdims=True)
    byte = np.maximum(np.where(amax > 0, np.frexp(amax)[1] - 1 + 127, 0) - down, 1)
    scale = np.exp2(byte - 127.0)
    codes = (blocks / scale).astype(np.float32).astype(dtype).astype(np.float64)
    return np.moveaxis((codes * scale).reshape(v.shape), -1, axis)


WIDE = False


def mx_kscale(k):
    if not WIDE:
        return np.ones(k)
    levels = np.array([10, -10, 5, -5, 0])
    if k % 512:
        return np.exp2(np.random.permutation(np.resize(levels, k // 32))).repeat(32)
    a = np.empty((k // 512, 16))
    for p in range(k // 512):
        a[p, :8] = np.random.permutation(np.resize(levels, 8))
        for g in range(8):
            far = levels[np.abs(levels - a[p, g]) >= 10]
            a[p, g + 8] = far[np.random.randint(len(far))]
    return np.exp2(a.ravel()).repeat(32)


def f64(x):
    return np.asarray(x).astype(np.float64)


def striped(idx):
    return np.tile(idx.reshape(-1, 16).T, (8, 1)).astype(np.uint16)


def unstriped(offs):
    return offs[:16].T.reshape(-1).astype(np.int64)


E2M1 = np.array([0.0, 0.5, 1.0, 1.5, 2.0, 3.0, 4.0, 6.0, -0.0, -0.5, -1.0, -1.5, -2.0, -3.0, -4.0, -6.0])


def pack_weight(w, fmt):
    k, n = w.shape
    w = f64(np.asarray(w, np.float32).astype(ml_dtypes.bfloat16)).reshape(k // 32, 32, n)
    amax = np.abs(w).max(1)
    if fmt == "e4m3":
        byte = np.frexp(amax)[1] - 1 + 127 - 7
    else:
        mant, ex = np.frexp(amax / 6.0)
        byte = np.where(mant > 0.5, ex, ex - 1) + 127
    byte = np.clip(np.where(amax > 0, byte, 1), 1, 254)
    scaled = (w * np.exp2(127.0 - byte)[:, None, :]).reshape(k, n).astype(np.float32)
    by_word = np.ascontiguousarray(scaled.reshape(k // 512, 128, 4, n).transpose(0, 1, 3, 2))
    if fmt == "e4m3":
        words = by_word.astype(ml_dtypes.float8_e4m3fn).view(np.uint8)
    else:
        c = by_word.astype(ml_dtypes.float4_e2m1fn).view(np.uint8) & 0xF
        words = (c[..., 0::2] | (c[..., 1::2] << 4)).reshape(k // 512, 128, 2 * n)
    return np.ascontiguousarray(words), np.ascontiguousarray(byte.astype(np.uint8).reshape(k // 512, 16, n))


def unpack_weight(words, scales, fmt):
    g, _, n = scales.shape
    words = np.ascontiguousarray(words).reshape(g, 128, n, -1)
    if fmt == "e4m3":
        vals = words.view(ml_dtypes.float8_e4m3fn).astype(np.float64)
    else:
        nib = np.empty((g, 128, n, 4), np.uint8)
        nib[..., 0::2] = words & 0xF
        nib[..., 1::2] = words >> 4
        vals = E2M1[nib]
    vals = vals * np.repeat(np.exp2(scales.astype(np.float64) - 127.0), 8, axis=1)[..., None]
    return vals.transpose(0, 1, 3, 2).reshape(g * 512, n)


def gelu(v):
    return 0.5 * v * (1.0 + np.tanh(np.sqrt(2.0 / np.pi) * (v + 0.044715 * v**3)))


K, A, B, H, T, S, T2, S2 = 1536, 512, 1024, 512, 2048, 1024, 4096, 1024

def setup_inputs():
    n = np.random.standard_normal
    s = mx_kscale(K)[:, None]
    u = mx_kscale(H)[:, None]
    tab_words, tab_scales = pack_weight(n((K, T)) * s, "e4m3")
    impacts = 0.5 * np.maximum(n((H, T2)), 0.0) ** 3 / np.sqrt(H)
    tab2_words, tab2_scales = pack_weight(impacts / u, "e4m3")
    w1 = n((A, H)) / np.sqrt(A) / s[:A]
    w4_words, w4_scales = pack_weight(n((B, H)) / np.sqrt(B) / s[A:], "e2m1")
    return {
        "tab_words": tab_words, "tab_scales": tab_scales,
        "tab2_words": tab2_words, "tab2_scales": tab2_scales,
        "w1": w1.astype(np.float32),
        "w4_words": w4_words, "w4_scales": w4_scales,
        "g": (np.exp(0.3 * n(H)) * u[:, 0]).astype(np.float32),
        "prior": (0.3 * n(S2)).astype(np.float32),
        "offs": striped(np.random.permutation(T)[:S]),
        "offs2": striped(np.random.permutation(T2)[:S2]),
    }

def reference(tab_words, tab_scales, tab2_words, tab2_scales, w1, w4_words, w4_scales, g, prior, offs, offs2):
    v = unpack_weight(tab_words, tab_scales, "e4m3")[:, unstriped(offs)]
    v2 = unpack_weight(tab2_words, tab2_scales, "e4m3")[:, unstriped(offs2)]
    w1q = mxq(f64(w1), 0, "e4m3")
    w4 = unpack_weight(w4_words, w4_scales, "e2m1")
    p = w1q.T @ v[:A] + w4.T @ v[A:]
    h = np.log(1.0 + np.maximum(p, 0.0)) * f64(g)[:, None]
    hq = mxq(h, 0, "e4m3")
    return (v2.T @ hq) + f64(prior)[:, None]

@@ -1,0 +1,215 @@
+from contextlib import ExitStack
+
+import concourse.mybir as mybir
+from concourse.masks import make_identity
+
+F32 = mybir.dt.float32
+BF16 = mybir.dt.bfloat16
+I32 = mybir.dt.int32
+U32 = mybir.dt.uint32
+U16 = mybir.dt.uint16
+U8 = mybir.dt.uint8
+FP8X4 = mybir.dt.float8_e4m3fn_x4
+FP4X4 = mybir.dt.float4_e2m1fn_x4
+ACT = mybir.ActivationFunctionType
+ALU = mybir.AluOpType
+
+P = 128
+H, T, S, T2, S2 = 512, 2048, 1024, 4096, 1024
+HALF = 512
+CHUNK = 256
+FLOPS = 2 * 1536 * H * S + 2 * H * S2 * S
+
+
+def tile_list_sparse_lexical_scores_kernel(
+    tc, tab_words, tab_scales, tab2_words, tab2_scales, w1, w4_words, w4_scales, g, prior, offs, offs2, out
+):
+    nc = tc.nc
+    with ExitStack() as ctx:
+        keep = ctx.enter_context(tc.tile_pool(name="keep", bufs=1))
+        work = ctx.enter_context(tc.tile_pool(name="work", bufs=2))
+        stage = ctx.enter_context(tc.tile_pool(name="stage", bufs=8))
+        psum = ctx.enter_context(tc.psum_pool(name="psum", bufs=8))
+
+        idx = keep.tile([P, S // 16], U16)
+        idx2 = keep.tile([P, S2 // 16], U16)
+        words = [keep.tile([P, T], I32, name=f"words{a}", align_bytes=64) for a in range(3)]
+        words2 = keep.tile([P, T2], I32, align_bytes=64)
+        planes = keep.tile([P, T // 4], I32, align_bytes=64)
+        plane2 = keep.tile([P, T2 // 4], I32, align_bytes=64)
+        w4_raw = keep.tile([P, 2, H // 2], I32, align_bytes=64)
+        w4s_raw = keep.tile([P, 2, H // 4], I32, align_bytes=64)
+        w1_raw = keep.tile([P, 4, H], F32, align_bytes=64)
+        gain = keep.tile([P, 2, 2], F32)
+        prior_rows = keep.tile([P, P], F32)
+        ident = keep.tile([P, P], F32)
+        prior_cols = keep.tile([P, S2 // P], F32)
+        v_planes = keep.tile([P, 3, S // 4], I32, align_bytes=64)
+        warm = keep.tile([P, 2], F32)
+
+        nc.vector.memset(w4s_raw[:], 0)
+        nc.vector.memset(warm[:, 0:1], 0.0)
+        nc.vector.memset(prior_rows[:], 0.0)
+        nc.vector.memset(plane2[:], 0)
+        for q in range(4):
+            nc.vector.memset(planes[32 * q : 32 * q + 20, :], 0)
+        nc.vector.memset(v_planes[96:P], 0)
+
+        def load_words(a):
+            nc.sync.dma_start(words[a][:], tab_words[a].rearrange("p t i -> p (t i)").bitcast(I32))
+
+        nc.sync.dma_start(idx[:], offs)
+        load_words(1)
+        for q in range(4):
+            nc.scalar.dma_start(planes[32 * q + 20 : 32 * q + 32, :], tab_scales[:, 4 * q : 4 * q + 4, :].bitcast(I32))
+        nc.sync.dma_start(w4_raw[:], w4_words.rearrange("a p n -> p a n").bitcast(I32))
+        nc.sync.dma_start(w1_raw[:], w1.rearrange("(p j) c -> p j c", j=4))
+        load_words(2)
+        for q in range(4):
+            nc.gpsimd.dma_start(
+                w4s_raw[32 * q : 32 * q + 4], w4_scales[:, 4 * q : 4 * q + 4, :].rearrange("a r n -> r a n").bitcast(I32)
+            )
+        load_words(0)
+        nc.sync.dma_start(idx2[:], offs2)
+        nc.sync.dma_start(words2[:], tab2_words[0].rearrange("p t i -> p (t i)").bitcast(I32))
+        nc.gpsimd.dma_start(prior_rows[0 : S2 // P, :], prior.rearrange("(m p) -> m p", p=P))
+        nc.gpsimd.dma_start(gain[:], g.rearrange("(p u e) -> p u e", u=2, e=2))
+        for q in range(4):
+            nc.gpsimd.dma_start(plane2[32 * q : 32 * q + 4, :], tab2_scales[0, 4 * q : 4 * q + 4, :].bitcast(I32))
+
+        nc.scalar.activation(warm[:, 1:2], warm[:, 0:1], ACT.Ln, bias=1.0)
+        make_identity(nc, ident[:])
+        prior_bank = psum.tile([P, HALF], F32, tag="bank", name="prior_bank")
+        nc.tensor.transpose(prior_bank[:, 0:P], prior_rows[:], ident[:])
+        nc.scalar.activation(prior_cols[:], prior_bank[:, 0 : S2 // P], ACT.Identity)
+
+        v_scales = keep.tile([P, S], U8, align_bytes=64)
+        nc.vector.tensor_copy(v_scales[:], planes[:].bitcast(U8).indirect(idx[:]))
+        for a in (1, 2, 0):
+            nc.sync.dma_start(v_planes[0:100, a, :], v_scales[4 * a + 20 : 4 * a + 120, :].bitcast(I32))
+
+        v_codes = [keep.tile([P, S], U32, name=f"v_codes{a}", align_bytes=64) for a in range(3)]
+        v2_codes = keep.tile([P, S2], U32, align_bytes=64)
+        v2_scales = keep.tile([P, S2], U8, align_bytes=64)
+
+        def cols(half):
+            return slice(half * HALF, (half + 1) * HALF)
+
+        def list_cols(half):
+            return slice(half * HALF // 16, (half + 1) * HALF // 16)
+
+        def gather_words(a, half):
+            nc.vector.tensor_copy(v_codes[a][:, cols(half)], words[a][:].bitcast(U32).indirect(idx[:, list_cols(half)]))
+
+        def gather_docs(half):
+            picks = idx2[:, list_cols(half)]
+            nc.vector.tensor_copy(v2_scales[:, cols(half)], plane2[:].bitcast(U8).indirect(picks))
+            nc.vector.tensor_copy(v2_codes[:, cols(half)], words2[:].bitcast(U32).indirect(picks))
+
+        gather_words(1, 0)
+
+        w4_codes = keep.tile([P, 2, 2 * H], U8, align_bytes=64)
+        w4_planes = keep.tile([P, 2, H], U8, align_bytes=64)
+        nc.vector.tensor_copy(
+            w4_codes[:].bitcast(U16).rearrange("p a (t m) -> p a t m", t=4),
+            w4_raw[:].bitcast(U16).rearrange("p a (m t) -> p a t m", t=4),
+        )
+        nc.vector.tensor_copy(
+            w4_planes[:].rearrange("p a (t m) -> p a t m", t=4),
+            w4s_raw[:].bitcast(U8).rearrange("p a (m t) -> p a t m", t=4),
+        )
+
+        w1_bf = keep.tile([P, 4 * H], BF16, align_bytes=64)
+        w1_codes = keep.tile([P, H], U32, align_bytes=64)
+        w1_plane = keep.tile([P, H], U8, align_bytes=64)
+        nc.scalar.activation(
+            w1_bf[:].rearrange("p (t m j) -> p m j t", t=4, j=4),
+            w1_raw[:].rearrange("p j (m t) -> p m j t", t=4),
+            ACT.Identity,
+        )
+        gather_words(2, 0)
+        nc.vector.quantize_mx(out=w1_codes[:].bitcast(FP8X4), scales=w1_plane[:], in_=w1_bf[:])
+        gather_words(0, 0)
+
+        def logits(half):
+            banks = [psum.tile([P, HALF], F32, tag="bank", name=f"logit{half}{t}") for t in range(4)]
+            for a in range(2):
+                for t in range(4):
+                    nc.tensor.matmul_mx(
+                        out=banks[t][:],
+                        lhsT=w4_codes[:, a, 2 * P * t : 2 * P * (t + 1)].bitcast(FP4X4),
+                        lhsT_scale=w4_planes[:, a, P * t : P * (t + 1)],
+                        rhs=v_codes[a + 1][:, cols(half)].bitcast(FP8X4),
+                        rhs_scale=v_planes[:, a + 1, :].bitcast(U8)[:, cols(half)],
+                        start=(a == 0),
+                        stop=False,
+                    )
+            for t in range(4):
+                nc.tensor.matmul_mx(
+                    out=banks[t][:],
+                    lhsT=w1_codes[:, P * t : P * (t + 1)].bitcast(FP8X4),
+                    lhsT_scale=w1_plane[:, P * t : P * (t + 1)],
+                    rhs=v_codes[0][:, cols(half)].bitcast(FP8X4),
+                    rhs_scale=v_planes[:, 0, :].bitcast(U8)[:, cols(half)],
+                    start=False,
+                    stop=True,
+                )
+            return banks
+
+        h_codes = keep.tile([P, S], U32, align_bytes=64)
+        h_scales = keep.tile([P, S], U8, align_bytes=64)
+
+        def term_weights(half, banks):
+            for c in range(HALF // CHUNK):
+                pos = work.tile([P, 2, 2, CHUNK], F32, name="pos")
+                for t in range(4):
+                    nc.scalar.activation(pos[:, t // 2, t % 2, :], banks[t][:, c * CHUNK : (c + 1) * CHUNK], ACT.Relu)
+                logs = work.tile([P, 2, CHUNK, 2], F32, name="logs")
+                nc.scalar.activation(logs[:], pos[:].rearrange("p u e n -> p u n e"), ACT.Ln, bias=1.0)
+                h_bf = work.tile([P, CHUNK, 2, 2], BF16, name="h_bf", align_bytes=64)
+                nc.vector.tensor_tensor(
+                    h_bf[:],
+                    logs[:].rearrange("p u n e -> p n u e"),
+                    gain[:].unsqueeze(1).to_broadcast([P, CHUNK, 2, 2]),
+                    ALU.mult,
+                )
+                at = slice(half * HALF + c * CHUNK, half * HALF + (c + 1) * CHUNK)
+                nc.vector.quantize_mx(
+                    out=h_codes[:, at].bitcast(FP8X4),
+                    scales=h_scales[:, at],
+                    in_=h_bf[:].rearrange("p n u e -> p (n u e)"),
+                )
+
+        def scores(m, half, on_vector):
+            bank = psum.tile([P, HALF], F32, tag="bank", name=f"score{m}{half}")
+            rows = slice(m * P, (m + 1) * P)
+            nc.tensor.matmul_mx(
+                out=bank[:],
+                lhsT=v2_codes[:, rows].bitcast(FP8X4),
+                lhsT_scale=v2_scales[:, rows],
+                rhs=h_codes[:, cols(half)].bitcast(FP8X4),
+                rhs_scale=h_scales[:, cols(half)],
+                start=True,
+                stop=True,
+            )
+            result = stage.tile([P, HALF], F32, name="result")
+            if on_vector:
+                nc.vector.tensor_scalar(result[:], bank[:], prior_cols[:, m : m + 1], None, ALU.add)
+            else:
+                nc.scalar.activation(result[:], bank[:], ACT.Identity, bias=prior_cols[:, m : m + 1])
+            nc.sync.dma_start(out[rows, cols(half)], result[:])
+
+        banks0 = logits(0)
+        term_weights(0, banks0)
+        for a in (1, 2, 0):
+            gather_words(a, 1)
+        banks1 = logits(1)
+        gather_docs(0)
+        for m in range(4):
+            scores(m, 0, False)
+        term_weights(1, banks1)
+        gather_docs(1)
+        for m in range(4, 8):
+            scores(m, 0, False)
+        for m in range(8):
+            scores(m, 1, m % 2 == 1)

@@ -1,7 +1,6 @@
 from contextlib import ExitStack
 
 import concourse.mybir as mybir
-from concourse.masks import make_identity
 
 F32 = mybir.dt.float32
 BF16 = mybir.dt.bfloat16
@@ -27,70 +26,69 @@ def tile_list_sparse_lexical_scores_kernel(
     nc = tc.nc
     with ExitStack() as ctx:
         keep = ctx.enter_context(tc.tile_pool(name="keep", bufs=1))
-        work = ctx.enter_context(tc.tile_pool(name="work", bufs=2))
+        work = ctx.enter_context(tc.tile_pool(name="work", bufs=4))
         stage = ctx.enter_context(tc.tile_pool(name="stage", bufs=8))
         psum = ctx.enter_context(tc.psum_pool(name="psum", bufs=8))
 
         idx = keep.tile([P, S // 16], U16)
         idx2 = keep.tile([P, S2 // 16], U16)
-        words = [keep.tile([P, T], I32, name=f"words{a}", align_bytes=64) for a in range(3)]
-        words2 = keep.tile([P, T2], I32, align_bytes=64)
-        planes = keep.tile([P, T // 4], I32, align_bytes=64)
+        words = [keep.tile([P, T], I32, name=f"words{a}", tag=f"words{a}", align_bytes=64) for a in range(3)]
+        planes = keep.tile([P, T // 4], I32, align_bytes=64, tag="planes_then_w4_planes")
         plane2 = keep.tile([P, T2 // 4], I32, align_bytes=64)
         w4_raw = keep.tile([P, 2, H // 2], I32, align_bytes=64)
-        w4s_raw = keep.tile([P, 2, H // 4], I32, align_bytes=64)
+        w4s_raw = keep.tile([P, 2, H // 4], I32, align_bytes=64, tag="w4s_then_words2")
         w1_raw = keep.tile([P, 4, H], F32, align_bytes=64)
         gain = keep.tile([P, 2, 2], F32)
-        prior_rows = keep.tile([P, P], F32)
-        ident = keep.tile([P, P], F32)
+        prior_rows = keep.tile([P, 32], F32, align_bytes=64)
+        prior_turned = keep.tile([P, 32], F32, align_bytes=64)
         prior_cols = keep.tile([P, S2 // P], F32)
-        v_planes = keep.tile([P, 3, S // 4], I32, align_bytes=64)
+        v_planes = keep.tile([P, 2, S // 4], I32, align_bytes=64)
         warm = keep.tile([P, 2], F32)
 
-        nc.vector.memset(w4s_raw[:], 0)
+        nc.gpsimd.memset(planes[:, 0 : T // 8], 0)
+        nc.vector.memset(planes[:, T // 8 : T // 4], 0)
+        nc.gpsimd.memset(w4s_raw[:], 0)
         nc.vector.memset(warm[:, 0:1], 0.0)
-        nc.vector.memset(prior_rows[:], 0.0)
         nc.vector.memset(plane2[:], 0)
-        for q in range(4):
-            nc.vector.memset(planes[32 * q : 32 * q + 20, :], 0)
         nc.vector.memset(v_planes[96:P], 0)
 
         def load_words(a):
             nc.sync.dma_start(words[a][:], tab_words[a].rearrange("p t i -> p (t i)").bitcast(I32))
 
+        def load_planes(queue, q):
+            queue.dma_start(planes[32 * q : 32 * q + 12, :], tab_scales[:, 4 * q : 4 * q + 4, :].bitcast(I32))
+
         nc.sync.dma_start(idx[:], offs)
+        nc.sync.dma_start(idx2[:], offs2)
+        nc.sync.dma_start(prior_rows[:], prior.rearrange("(r b) -> r b", b=32).unsqueeze(0).to_broadcast([4, 32, 32]))
+        nc.sync.dma_start(gain[:], g.rearrange("(p u e) -> p u e", u=2, e=2))
         load_words(1)
-        for q in range(4):
-            nc.scalar.dma_start(planes[32 * q + 20 : 32 * q + 32, :], tab_scales[:, 4 * q : 4 * q + 4, :].bitcast(I32))
+        load_planes(nc.scalar, 0)
+        load_planes(nc.sync, 1)
+        load_planes(nc.scalar, 2)
+        load_planes(nc.sync, 3)
         nc.sync.dma_start(w4_raw[:], w4_words.rearrange("a p n -> p a n").bitcast(I32))
-        nc.sync.dma_start(w1_raw[:], w1.rearrange("(p j) c -> p j c", j=4))
         load_words(2)
+        nc.sync.dma_start(w1_raw[:], w1.rearrange("(p j) c -> p j c", j=4))
+        load_words(0)
         for q in range(4):
             nc.gpsimd.dma_start(
                 w4s_raw[32 * q : 32 * q + 4], w4_scales[:, 4 * q : 4 * q + 4, :].rearrange("a r n -> r a n").bitcast(I32)
             )
-        load_words(0)
-        nc.sync.dma_start(idx2[:], offs2)
-        nc.sync.dma_start(words2[:], tab2_words[0].rearrange("p t i -> p (t i)").bitcast(I32))
-        nc.gpsimd.dma_start(prior_rows[0 : S2 // P, :], prior.rearrange("(m p) -> m p", p=P))
-        nc.gpsimd.dma_start(gain[:], g.rearrange("(p u e) -> p u e", u=2, e=2))
         for q in range(4):
             nc.gpsimd.dma_start(plane2[32 * q : 32 * q + 4, :], tab2_scales[0, 4 * q : 4 * q + 4, :].bitcast(I32))
-
         nc.scalar.activation(warm[:, 1:2], warm[:, 0:1], ACT.Ln, bias=1.0)
-        make_identity(nc, ident[:])
-        prior_bank = psum.tile([P, HALF], F32, tag="bank", name="prior_bank")
-        nc.tensor.transpose(prior_bank[:, 0:P], prior_rows[:], ident[:])
-        nc.scalar.activation(prior_cols[:], prior_bank[:, 0 : S2 // P], ACT.Identity)
+        nc.vector.transpose(prior_turned[:], prior_rows[:])
+        for q in range(4):
+            nc.vector.tensor_copy(prior_cols[32 * q : 32 * q + 32, :], prior_turned[32 * q : 32 * q + 32, q : 32 : 4])
 
         v_scales = keep.tile([P, S], U8, align_bytes=64)
-        nc.vector.tensor_copy(v_scales[:], planes[:].bitcast(U8).indirect(idx[:]))
-        for a in (1, 2, 0):
-            nc.sync.dma_start(v_planes[0:100, a, :], v_scales[4 * a + 20 : 4 * a + 120, :].bitcast(I32))
-
-        v_codes = [keep.tile([P, S], U32, name=f"v_codes{a}", align_bytes=64) for a in range(3)]
-        v2_codes = keep.tile([P, S2], U32, align_bytes=64)
-        v2_scales = keep.tile([P, S2], U8, align_bytes=64)
+        v_codes = {
+            (a, half): keep.tile([P, HALF], U32, name=f"v_codes{a}{half}", tag=f"v_codes{a}{half}", align_bytes=64)
+            for a in range(3)
+            for half in range(2)
+            if (a, half) != (0, 1)
+        }
 
         def cols(half):
             return slice(half * HALF, (half + 1) * HALF)
@@ -99,117 +97,138 @@ def tile_list_sparse_lexical_scores_kernel(
             return slice(half * HALF // 16, (half + 1) * HALF // 16)
 
         def gather_words(a, half):
-            nc.vector.tensor_copy(v_codes[a][:, cols(half)], words[a][:].bitcast(U32).indirect(idx[:, list_cols(half)]))
+            nc.vector.tensor_copy(v_codes[a, half][:], words[a][:].bitcast(U32).indirect(idx[:, list_cols(half)]))
 
-        def gather_docs(half):
-            picks = idx2[:, list_cols(half)]
-            nc.vector.tensor_copy(v2_scales[:, cols(half)], plane2[:].bitcast(U8).indirect(picks))
-            nc.vector.tensor_copy(v2_codes[:, cols(half)], words2[:].bitcast(U32).indirect(picks))
+        def gather_doc_scales(half):
+            nc.vector.tensor_copy(v2_scales[:, cols(half)], plane2[:].bitcast(U8).indirect(idx2[:, list_cols(half)]))
+
+        def gather_doc_words(half):
+            nc.vector.tensor_copy(v2_codes[:, cols(half)], words2[:].bitcast(U32).indirect(idx2[:, list_cols(half)]))
 
         gather_words(1, 0)
+        nc.vector.tensor_copy(v_scales[:], planes[:].bitcast(U8).indirect(idx[:]))
+        for a in (1, 2):
+            nc.scalar.dma_start(v_planes[0:100, a - 1, :], v_scales[4 * a : 4 * a + 100, :].bitcast(I32))
+        gather_words(2, 0)
 
         w4_codes = keep.tile([P, 2, 2 * H], U8, align_bytes=64)
-        w4_planes = keep.tile([P, 2, H], U8, align_bytes=64)
-        nc.vector.tensor_copy(
-            w4_codes[:].bitcast(U16).rearrange("p a (t m) -> p a t m", t=4),
-            w4_raw[:].bitcast(U16).rearrange("p a (m t) -> p a t m", t=4),
-        )
+        w4_planes = keep.tile([P, 2, H], U8, align_bytes=64, tag="planes_then_w4_planes")
         nc.vector.tensor_copy(
             w4_planes[:].rearrange("p a (t m) -> p a t m", t=4),
             w4s_raw[:].bitcast(U8).rearrange("p a (m t) -> p a t m", t=4),
         )
+        words2 = keep.tile([P, T2], I32, align_bytes=64, tag="w4s_then_words2")
+        nc.sync.dma_start(words2[:], tab2_words[0].rearrange("p t i -> p (t i)").bitcast(I32))
+        nc.vector.tensor_copy(
+            w4_codes[:].bitcast(U16).rearrange("p a (t m) -> p a t m", t=4),
+            w4_raw[:].bitcast(U16).rearrange("p a (m t) -> p a t m", t=4),
+        )
 
-        w1_bf = keep.tile([P, 4 * H], BF16, align_bytes=64)
+        w1_bf = keep.tile([P, 4 * H], BF16, tag="w1_bf_then_v2_codes", align_bytes=64)
         w1_codes = keep.tile([P, H], U32, align_bytes=64)
         w1_plane = keep.tile([P, H], U8, align_bytes=64)
-        nc.scalar.activation(
-            w1_bf[:].rearrange("p (t m j) -> p m j t", t=4, j=4),
-            w1_raw[:].rearrange("p j (m t) -> p m j t", t=4),
-            ACT.Identity,
-        )
-        gather_words(2, 0)
-        nc.vector.quantize_mx(out=w1_codes[:].bitcast(FP8X4), scales=w1_plane[:], in_=w1_bf[:])
-        gather_words(0, 0)
+        for u in range(2):
+            nc.scalar.activation(
+                w1_bf[:].rearrange("p (t m j) -> p m j t", t=4, j=4)[:, :, :, 2 * u : 2 * u + 2],
+                w1_raw[:].rearrange("p j (m t) -> p m j t", t=4)[:, :, :, 2 * u : 2 * u + 2],
+                ACT.Identity,
+            )
 
-        def logits(half):
+        def quantize_w1(u):
+            at = slice(2 * P * u, 2 * P * (u + 1))
+            nc.vector.quantize_mx(
+                out=w1_codes[:, at].bitcast(FP8X4), scales=w1_plane[:, at], in_=w1_bf[:, 8 * P * u : 8 * P * (u + 1)]
+            )
+
+        gather_words(1, 1)
+        gather_words(2, 1)
+        quantize_w1(0)
+        gather_words(0, 0)
+        quantize_w1(1)
+
+        def logits(half, order):
             banks = [psum.tile([P, HALF], F32, tag="bank", name=f"logit{half}{t}") for t in range(4)]
-            for a in range(2):
+            for a in order:
                 for t in range(4):
+                    if a == 0:
+                        weights = w1_codes[:, P * t : P * (t + 1)].bitcast(FP8X4)
+                        weight_scales = w1_plane[:, P * t : P * (t + 1)]
+                    else:
+                        weights = w4_codes[:, a - 1, 2 * P * t : 2 * P * (t + 1)].bitcast(FP4X4)
+                        weight_scales = w4_planes[:, a - 1, P * t : P * (t + 1)]
                     nc.tensor.matmul_mx(
                         out=banks[t][:],
-                        lhsT=w4_codes[:, a, 2 * P * t : 2 * P * (t + 1)].bitcast(FP4X4),
-                        lhsT_scale=w4_planes[:, a, P * t : P * (t + 1)],
-                        rhs=v_codes[a + 1][:, cols(half)].bitcast(FP8X4),
-                        rhs_scale=v_planes[:, a + 1, :].bitcast(U8)[:, cols(half)],
-                        start=(a == 0),
-                        stop=False,
+                        lhsT=weights,
+                        lhsT_scale=weight_scales,
+                        rhs=v_codes[a, half][:].bitcast(FP8X4),
+                        rhs_scale=(v_planes[:, a - 1, :].bitcast(U8) if a else v_scales)[:, cols(half)],
+                        start=(a == order[0]),
+                        stop=(a == order[-1]),
                     )
-            for t in range(4):
-                nc.tensor.matmul_mx(
-                    out=banks[t][:],
-                    lhsT=w1_codes[:, P * t : P * (t + 1)].bitcast(FP8X4),
-                    lhsT_scale=w1_plane[:, P * t : P * (t + 1)],
-                    rhs=v_codes[0][:, cols(half)].bitcast(FP8X4),
-                    rhs_scale=v_planes[:, 0, :].bitcast(U8)[:, cols(half)],
-                    start=False,
-                    stop=True,
-                )
             return banks
 
-        h_codes = keep.tile([P, S], U32, align_bytes=64)
         h_scales = keep.tile([P, S], U8, align_bytes=64)
 
-        def term_weights(half, banks):
-            for c in range(HALF // CHUNK):
-                pos = work.tile([P, 2, 2, CHUNK], F32, name="pos")
-                for t in range(4):
-                    nc.scalar.activation(pos[:, t // 2, t % 2, :], banks[t][:, c * CHUNK : (c + 1) * CHUNK], ACT.Relu)
-                logs = work.tile([P, 2, CHUNK, 2], F32, name="logs")
-                nc.scalar.activation(logs[:], pos[:].rearrange("p u e n -> p u n e"), ACT.Ln, bias=1.0)
-                h_bf = work.tile([P, CHUNK, 2, 2], BF16, name="h_bf", align_bytes=64)
-                nc.vector.tensor_tensor(
-                    h_bf[:],
-                    logs[:].rearrange("p u n e -> p n u e"),
-                    gain[:].unsqueeze(1).to_broadcast([P, CHUNK, 2, 2]),
-                    ALU.mult,
-                )
-                at = slice(half * HALF + c * CHUNK, half * HALF + (c + 1) * CHUNK)
-                nc.vector.quantize_mx(
-                    out=h_codes[:, at].bitcast(FP8X4),
-                    scales=h_scales[:, at],
-                    in_=h_bf[:].rearrange("p n u e -> p (n u e)"),
-                )
-
-        def scores(m, half, on_vector):
-            bank = psum.tile([P, HALF], F32, tag="bank", name=f"score{m}{half}")
-            rows = slice(m * P, (m + 1) * P)
-            nc.tensor.matmul_mx(
-                out=bank[:],
-                lhsT=v2_codes[:, rows].bitcast(FP8X4),
-                lhsT_scale=v2_scales[:, rows],
-                rhs=h_codes[:, cols(half)].bitcast(FP8X4),
-                rhs_scale=h_scales[:, cols(half)],
-                start=True,
-                stop=True,
+        def term_weights(c, banks):
+            inside = slice(c % 2 * CHUNK, (c % 2 + 1) * CHUNK)
+            pos = work.tile([P, 2, 2, CHUNK], F32, name="pos", bufs=1)
+            for t in range(4):
+                nc.scalar.activation(pos[:, t // 2, t % 2, :], banks[t][:, inside], ACT.Relu)
+            logs = work.tile([P, 2, CHUNK, 2], F32, name="logs")
+            nc.scalar.activation(logs[:], pos[:].rearrange("p u e n -> p u n e"), ACT.Ln, bias=1.0)
+            h_bf = work.tile([P, CHUNK, 2, 2], BF16, name="h_bf", align_bytes=64)
+            nc.gpsimd.tensor_tensor(
+                h_bf[:],
+                logs[:].rearrange("p u n e -> p n u e"),
+                gain[:].unsqueeze(1).to_broadcast([P, CHUNK, 2, 2]),
+                ALU.mult,
             )
-            result = stage.tile([P, HALF], F32, name="result")
-            if on_vector:
-                nc.vector.tensor_scalar(result[:], bank[:], prior_cols[:, m : m + 1], None, ALU.add)
-            else:
-                nc.scalar.activation(result[:], bank[:], ACT.Identity, bias=prior_cols[:, m : m + 1])
-            nc.sync.dma_start(out[rows, cols(half)], result[:])
+            at = slice(c * CHUNK, (c + 1) * CHUNK)
+            nc.vector.quantize_mx(
+                out=h_codes[:, at].bitcast(FP8X4),
+                scales=h_scales[:, at],
+                in_=h_bf[:].rearrange("p n u e -> p (n u e)"),
+            )
 
-        banks0 = logits(0)
-        term_weights(0, banks0)
-        for a in (1, 2, 0):
-            gather_words(a, 1)
-        banks1 = logits(1)
-        gather_docs(0)
-        for m in range(4):
-            scores(m, 0, False)
-        term_weights(1, banks1)
-        gather_docs(1)
-        for m in range(4, 8):
-            scores(m, 0, False)
-        for m in range(8):
-            scores(m, 1, m % 2 == 1)
+        def scores(m0, count, at, on_vector):
+            width = HALF // count
+            bank = psum.tile([P, count, width], F32, tag="bank", name=f"score{m0}_{at.start}")
+            for i in range(count):
+                rows = slice((m0 + i) * P, (m0 + i + 1) * P)
+                nc.tensor.matmul_mx(
+                    out=bank[:, i, :],
+                    lhsT=v2_codes[:, rows].bitcast(FP8X4),
+                    lhsT_scale=v2_scales[:, rows],
+                    rhs=h_codes[:, at].bitcast(FP8X4),
+                    rhs_scale=h_scales[:, at],
+                    start=True,
+                    stop=True,
+                )
+            result = stage.tile([P, count, width], F32, name="result")
+            if on_vector:
+                nc.vector.tensor_tensor(
+                    result[:], bank[:], prior_cols[:, m0 : m0 + count].unsqueeze(2).to_broadcast([P, count, width]), ALU.add
+                )
+            else:
+                for i in range(count):
+                    nc.scalar.activation(result[:, i, :], bank[:, i, :], ACT.Identity, bias=prior_cols[:, m0 + i : m0 + i + 1])
+            nc.sync.dma_start(out[m0 * P : (m0 + count) * P, at].rearrange("(i p) n -> p i n", p=P), result[:])
+
+        def chunk(c):
+            return slice(c * CHUNK, (c + 1) * CHUNK)
+
+        banks0 = logits(0, (1, 2, 0))
+        v_codes[0, 1] = keep.tile([P, HALF], U32, name="v_codes01", tag="v_codes20", align_bytes=64)
+        gather_words(0, 1)
+        banks1 = logits(1, (0, 1, 2))
+        v2_scales = keep.tile([P, S2], U8, tag="w1_bf_then_v2_codes", align_bytes=64)
+        v2_codes = keep.tile([P, S2], U32, tag="words0", align_bytes=64)
+        for half in range(2):
+            gather_doc_scales(half)
+            gather_doc_words(half)
+        h_codes = keep.tile([P, S], U32, tag="w4s_then_words2", align_bytes=64)
+        for c in range(4):
+            term_weights(c, (banks0, banks1)[c // 2])
+        for c in range(4):
+            for m0 in (0, 2, 4, 6):
+                scores(m0, 2, chunk(c), c < 2 or (c, m0) in ((3, 2), (3, 6)))

@@ -33,11 +33,10 @@ def tile_list_sparse_lexical_scores_kernel(
         idx = keep.tile([P, S // 16], U16)
         idx2 = keep.tile([P, S2 // 16], U16)
         words = [keep.tile([P, T], I32, name=f"words{a}", tag=f"words{a}", align_bytes=64) for a in range(3)]
-        planes = keep.tile([P, T // 4], I32, align_bytes=64, tag="planes_then_w4_planes")
-        plane2 = keep.tile([P, T2 // 4], I32, align_bytes=64)
+        w1_raw = keep.tile([P, 4, H], F32, align_bytes=64)
+        planes = keep.tile([P, T // 4], I32, align_bytes=64)
         w4_raw = keep.tile([P, 2, H // 2], I32, align_bytes=64)
         w4s_raw = keep.tile([P, 2, H // 4], I32, align_bytes=64, tag="w4s_then_words2")
-        w1_raw = keep.tile([P, 4, H], F32, align_bytes=64)
         gain = keep.tile([P, 2, 2], F32)
         prior_rows = keep.tile([P, 32], F32, align_bytes=64)
         prior_turned = keep.tile([P, 32], F32, align_bytes=64)
@@ -45,23 +44,21 @@ def tile_list_sparse_lexical_scores_kernel(
         v_planes = keep.tile([P, 2, S // 4], I32, align_bytes=64)
         warm = keep.tile([P, 2], F32)
 
-        nc.gpsimd.memset(planes[:, 0 : T // 8], 0)
-        nc.vector.memset(planes[:, T // 8 : T // 4], 0)
-        nc.gpsimd.memset(w4s_raw[:], 0)
         nc.vector.memset(warm[:, 0:1], 0.0)
-        nc.vector.memset(plane2[:], 0)
-        nc.vector.memset(v_planes[96:P], 0)
+        nc.gpsimd.memset(w4s_raw[:], 0)
+        for q in range(4):
+            nc.vector.memset(planes[32 * q : 32 * q + 12, :], 0)
+        nc.gpsimd.memset(v_planes[96:P], 0)
 
         def load_words(a):
             nc.sync.dma_start(words[a][:], tab_words[a].rearrange("p t i -> p (t i)").bitcast(I32))
 
+        scale_rows = tab_scales.rearrange("a (h e r) n -> e (a h) r n", h=2, e=2)
+
         def load_planes(queue, q):
-            queue.dma_start(planes[32 * q : 32 * q + 12, :], tab_scales[:, 4 * q : 4 * q + 4, :].bitcast(I32))
+            queue.dma_start(planes[32 * q + 12 : 32 * q + 32, :], scale_rows[q % 2, q // 2 : q // 2 + 5].bitcast(I32))
 
         nc.sync.dma_start(idx[:], offs)
-        nc.sync.dma_start(idx2[:], offs2)
-        nc.sync.dma_start(prior_rows[:], prior.rearrange("(r b) -> r b", b=32).unsqueeze(0).to_broadcast([4, 32, 32]))
-        nc.sync.dma_start(gain[:], g.rearrange("(p u e) -> p u e", u=2, e=2))
         load_words(1)
         load_planes(nc.scalar, 0)
         load_planes(nc.sync, 1)
@@ -69,18 +66,14 @@ def tile_list_sparse_lexical_scores_kernel(
         load_planes(nc.sync, 3)
         nc.sync.dma_start(w4_raw[:], w4_words.rearrange("a p n -> p a n").bitcast(I32))
         load_words(2)
+        for r in range(4):
+            nc.sync.dma_start(w4s_raw[r:P:32], w4_scales[:, r:16:4, :].rearrange("a q n -> q a n").bitcast(I32))
         nc.sync.dma_start(w1_raw[:], w1.rearrange("(p j) c -> p j c", j=4))
         load_words(0)
-        for q in range(4):
-            nc.gpsimd.dma_start(
-                w4s_raw[32 * q : 32 * q + 4], w4_scales[:, 4 * q : 4 * q + 4, :].rearrange("a r n -> r a n").bitcast(I32)
-            )
-        for q in range(4):
-            nc.gpsimd.dma_start(plane2[32 * q : 32 * q + 4, :], tab2_scales[0, 4 * q : 4 * q + 4, :].bitcast(I32))
+        nc.sync.dma_start(idx2[:], offs2)
+        nc.sync.dma_start(gain[:], g.rearrange("(p u e) -> p u e", u=2, e=2))
+        nc.sync.dma_start(prior_rows[:], prior.rearrange("(r b) -> r b", b=32).unsqueeze(0).to_broadcast([4, 32, 32]))
         nc.scalar.activation(warm[:, 1:2], warm[:, 0:1], ACT.Ln, bias=1.0)
-        nc.vector.transpose(prior_turned[:], prior_rows[:])
-        for q in range(4):
-            nc.vector.tensor_copy(prior_cols[32 * q : 32 * q + 32, :], prior_turned[32 * q : 32 * q + 32, q : 32 : 4])
 
         v_scales = keep.tile([P, S], U8, align_bytes=64)
         v_codes = {
@@ -108,11 +101,11 @@ def tile_list_sparse_lexical_scores_kernel(
         gather_words(1, 0)
         nc.vector.tensor_copy(v_scales[:], planes[:].bitcast(U8).indirect(idx[:]))
         for a in (1, 2):
-            nc.scalar.dma_start(v_planes[0:100, a - 1, :], v_scales[4 * a : 4 * a + 100, :].bitcast(I32))
+            nc.scalar.dma_start(v_planes[0:100, a - 1, :], v_scales[8 * a + 12 : 8 * a + 112, :].bitcast(I32))
         gather_words(2, 0)
 
         w4_codes = keep.tile([P, 2, 2 * H], U8, align_bytes=64)
-        w4_planes = keep.tile([P, 2, H], U8, align_bytes=64, tag="planes_then_w4_planes")
+        w4_planes = keep.tile([P, 2, H], U8, align_bytes=64)
         nc.vector.tensor_copy(
             w4_planes[:].rearrange("p a (t m) -> p a t m", t=4),
             w4s_raw[:].bitcast(U8).rearrange("p a (m t) -> p a t m", t=4),
@@ -124,7 +117,7 @@ def tile_list_sparse_lexical_scores_kernel(
             w4_raw[:].bitcast(U16).rearrange("p a (m t) -> p a t m", t=4),
         )
 
-        w1_bf = keep.tile([P, 4 * H], BF16, tag="w1_bf_then_v2_codes", align_bytes=64)
+        w1_bf = keep.tile([P, 4 * H], BF16, align_bytes=64)
         w1_codes = keep.tile([P, H], U32, align_bytes=64)
         w1_plane = keep.tile([P, H], U8, align_bytes=64)
         for u in range(2):
@@ -141,7 +134,6 @@ def tile_list_sparse_lexical_scores_kernel(
             )
 
         gather_words(1, 1)
-        gather_words(2, 1)
         quantize_w1(0)
         gather_words(0, 0)
         quantize_w1(1)
@@ -161,12 +153,13 @@ def tile_list_sparse_lexical_scores_kernel(
                         lhsT=weights,
                         lhsT_scale=weight_scales,
                         rhs=v_codes[a, half][:].bitcast(FP8X4),
-                        rhs_scale=(v_planes[:, a - 1, :].bitcast(U8) if a else v_scales)[:, cols(half)],
+                        rhs_scale=(v_planes[:, a - 1, :].bitcast(U8) if a else v_scales[12:P])[:, cols(half)],
                         start=(a == order[0]),
                         stop=(a == order[-1]),
                     )
             return banks
 
+        h_codes = keep.tile([P, S], U32, align_bytes=64)
         h_scales = keep.tile([P, S], U8, align_bytes=64)
 
         def term_weights(c, banks):
@@ -176,8 +169,10 @@ def tile_list_sparse_lexical_scores_kernel(
                 nc.scalar.activation(pos[:, t // 2, t % 2, :], banks[t][:, inside], ACT.Relu)
             logs = work.tile([P, 2, CHUNK, 2], F32, name="logs")
             nc.scalar.activation(logs[:], pos[:].rearrange("p u e n -> p u n e"), ACT.Ln, bias=1.0)
-            h_bf = work.tile([P, CHUNK, 2, 2], BF16, name="h_bf", align_bytes=64)
-            nc.gpsimd.tensor_tensor(
+            h_bf = keep.tile(
+                [P, CHUNK, 2, 2], BF16, name=f"h_bf{c}", tag="w4s_then_words2" if c else "h_first", align_bytes=64
+            )
+            nc.vector.tensor_tensor(
                 h_bf[:],
                 logs[:].rearrange("p u n e -> p n u e"),
                 gain[:].unsqueeze(1).to_broadcast([P, CHUNK, 2, 2]),
@@ -218,17 +213,31 @@ def tile_list_sparse_lexical_scores_kernel(
             return slice(c * CHUNK, (c + 1) * CHUNK)
 
         banks0 = logits(0, (1, 2, 0))
+        plane2 = keep.tile([P, T2 // 4], I32, align_bytes=64, tag="v_codes10")
+        nc.gpsimd.memset(plane2[:], 0)
+        for r in range(4):
+            nc.sync.dma_start(plane2[r:P:32, :], tab2_scales[0, r:16:4, :].bitcast(I32))
+        nc.vector.transpose(prior_turned[:], prior_rows[:])
+        for q in range(4):
+            nc.vector.tensor_copy(prior_cols[32 * q : 32 * q + 32, :], prior_turned[32 * q : 32 * q + 32, q : 32 : 4])
+        gather_words(2, 1)
         v_codes[0, 1] = keep.tile([P, HALF], U32, name="v_codes01", tag="v_codes20", align_bytes=64)
         gather_words(0, 1)
         banks1 = logits(1, (0, 1, 2))
-        v2_scales = keep.tile([P, S2], U8, tag="w1_bf_then_v2_codes", align_bytes=64)
+        v2_scales = keep.tile([P, S2], U8, align_bytes=64)
         v2_codes = keep.tile([P, S2], U32, tag="words0", align_bytes=64)
-        for half in range(2):
-            gather_doc_scales(half)
-            gather_doc_words(half)
-        h_codes = keep.tile([P, S], U32, tag="w4s_then_words2", align_bytes=64)
-        for c in range(4):
-            term_weights(c, (banks0, banks1)[c // 2])
-        for c in range(4):
+        term_weights(0, banks0)
+        gather_doc_words(0)
+        gather_doc_scales(0)
+        scores(0, 2, chunk(0), True)
+        scores(2, 2, chunk(0), True)
+        gather_doc_words(1)
+        gather_doc_scales(1)
+        term_weights(1, banks0)
+        term_weights(2, banks1)
+        term_weights(3, banks1)
+        scores(4, 2, chunk(0), False)
+        scores(6, 2, chunk(0), False)
+        for c in range(1, 4):
             for m0 in (0, 2, 4, 6):
-                scores(m0, 2, chunk(c), c < 2 or (c, m0) in ((3, 2), (3, 6)))
+                scores(m0, 2, chunk(c), (c, m0) in ((2, 4), (2, 6), (3, 2), (3, 6)))

@@ -35,6 +35,7 @@ def tile_list_sparse_lexical_scores_kernel(
         words = [keep.tile([P, T], I32, name=f"words{a}", tag=f"words{a}", align_bytes=64) for a in range(3)]
         w1_raw = keep.tile([P, 4, H], F32, align_bytes=64)
         planes = keep.tile([P, T // 4], I32, align_bytes=64)
+        plane2 = keep.tile([P, T2 // 4], I32, align_bytes=64)
         w4_raw = keep.tile([P, 2, H // 2], I32, align_bytes=64)
         w4s_raw = keep.tile([P, 2, H // 4], I32, align_bytes=64, tag="w4s_then_words2")
         gain = keep.tile([P, 2, 2], F32)
@@ -48,7 +49,10 @@ def tile_list_sparse_lexical_scores_kernel(
         nc.gpsimd.memset(w4s_raw[:], 0)
         for q in range(4):
             nc.vector.memset(planes[32 * q : 32 * q + 12, :], 0)
-        nc.gpsimd.memset(v_planes[96:P], 0)
+        nc.vector.memset(v_planes[96:P], 0)
+        nc.gpsimd.memset(plane2[:], 0)
+        for r in range(4):
+            nc.gpsimd.dma_start(plane2[r:P:32, :], tab2_scales[0, r:16:4, :].bitcast(I32))
 
         def load_words(a):
             nc.sync.dma_start(words[a][:], tab_words[a].rearrange("p t i -> p (t i)").bitcast(I32))
@@ -117,7 +121,7 @@ def tile_list_sparse_lexical_scores_kernel(
             w4_raw[:].bitcast(U16).rearrange("p a (m t) -> p a t m", t=4),
         )
 
-        w1_bf = keep.tile([P, 4 * H], BF16, align_bytes=64)
+        w1_bf = keep.tile([P, 4 * H], BF16, tag="w1_bf_then_v2_codes", align_bytes=64)
         w1_codes = keep.tile([P, H], U32, align_bytes=64)
         w1_plane = keep.tile([P, H], U8, align_bytes=64)
         for u in range(2):
@@ -159,7 +163,6 @@ def tile_list_sparse_lexical_scores_kernel(
                     )
             return banks
 
-        h_codes = keep.tile([P, S], U32, align_bytes=64)
         h_scales = keep.tile([P, S], U8, align_bytes=64)
 
         def term_weights(c, banks):
@@ -169,10 +172,8 @@ def tile_list_sparse_lexical_scores_kernel(
                 nc.scalar.activation(pos[:, t // 2, t % 2, :], banks[t][:, inside], ACT.Relu)
             logs = work.tile([P, 2, CHUNK, 2], F32, name="logs")
             nc.scalar.activation(logs[:], pos[:].rearrange("p u e n -> p u n e"), ACT.Ln, bias=1.0)
-            h_bf = keep.tile(
-                [P, CHUNK, 2, 2], BF16, name=f"h_bf{c}", tag="w4s_then_words2" if c else "h_first", align_bytes=64
-            )
-            nc.vector.tensor_tensor(
+            h_bf = work.tile([P, CHUNK, 2, 2], BF16, name="h_bf", align_bytes=64)
+            nc.gpsimd.tensor_tensor(
                 h_bf[:],
                 logs[:].rearrange("p u n e -> p n u e"),
                 gain[:].unsqueeze(1).to_broadcast([P, CHUNK, 2, 2]),
@@ -213,10 +214,6 @@ def tile_list_sparse_lexical_scores_kernel(
             return slice(c * CHUNK, (c + 1) * CHUNK)
 
         banks0 = logits(0, (1, 2, 0))
-        plane2 = keep.tile([P, T2 // 4], I32, align_bytes=64, tag="v_codes10")
-        nc.gpsimd.memset(plane2[:], 0)
-        for r in range(4):
-            nc.sync.dma_start(plane2[r:P:32, :], tab2_scales[0, r:16:4, :].bitcast(I32))
         nc.vector.transpose(prior_turned[:], prior_rows[:])
         for q in range(4):
             nc.vector.tensor_copy(prior_cols[32 * q : 32 * q + 32, :], prior_turned[32 * q : 32 * q + 32, q : 32 : 4])
@@ -224,20 +221,14 @@ def tile_list_sparse_lexical_scores_kernel(
         v_codes[0, 1] = keep.tile([P, HALF], U32, name="v_codes01", tag="v_codes20", align_bytes=64)
         gather_words(0, 1)
         banks1 = logits(1, (0, 1, 2))
-        v2_scales = keep.tile([P, S2], U8, align_bytes=64)
-        v2_codes = keep.tile([P, S2], U32, tag="words0", align_bytes=64)
-        term_weights(0, banks0)
-        gather_doc_words(0)
-        gather_doc_scales(0)
-        scores(0, 2, chunk(0), True)
-        scores(2, 2, chunk(0), True)
-        gather_doc_words(1)
-        gather_doc_scales(1)
-        term_weights(1, banks0)
-        term_weights(2, banks1)
-        term_weights(3, banks1)
-        scores(4, 2, chunk(0), False)
-        scores(6, 2, chunk(0), False)
-        for c in range(1, 4):
+        v2_scales = keep.tile([P, S2], U8, tag="words0", align_bytes=64)
+        v2_codes = keep.tile([P, S2], U32, tag="w1_bf_then_v2_codes", align_bytes=64)
+        for half in range(2):
+            gather_doc_scales(half)
+        for half in range(2):
+            gather_doc_words(half)
+        h_codes = keep.tile([P, S], U32, tag="w4s_then_words2", align_bytes=64)
+        for c in range(4):
+            term_weights(c, (banks0, banks1)[c // 2])
             for m0 in (0, 2, 4, 6):
-                scores(m0, 2, chunk(c), (c, m0) in ((2, 4), (2, 6), (3, 2), (3, 6)))
+                scores(m0, 2, chunk(c), c < 2 or (c, m0) in ((3, 2), (3, 6)))

@@ -14,10 +14,18 @@ ACT = mybir.ActivationFunctionType
 ALU = mybir.AluOpType
 
 P = 128
-H, T, S, T2, S2 = 512, 2048, 1024, 4096, 1024
+QUAD = 32
+K, H = 1536, 512
+T, S = 2048, 1024
+T2, S2 = 4096, 1024
 HALF = 512
 CHUNK = 256
-FLOPS = 2 * 1536 * H * S + 2 * H * S2 * S
+LIST = 16
+FIRST_ROW = 12
+PASS_ROWS = 8
+PLANE_ROWS = 3 * QUAD + 4
+VECTOR_TILES = (0, 1, 2, 4, 6)
+FLOPS = 2 * K * H * S + 2 * H * S2 * S
 
 
 def tile_list_sparse_lexical_scores_kernel(
@@ -26,62 +34,60 @@ def tile_list_sparse_lexical_scores_kernel(
     nc = tc.nc
     with ExitStack() as ctx:
         keep = ctx.enter_context(tc.tile_pool(name="keep", bufs=1))
-        work = ctx.enter_context(tc.tile_pool(name="work", bufs=4))
-        stage = ctx.enter_context(tc.tile_pool(name="stage", bufs=8))
+        work = ctx.enter_context(tc.tile_pool(name="work", bufs=S // CHUNK))
+        stage = ctx.enter_context(tc.tile_pool(name="stage", bufs=S2 // P))
         psum = ctx.enter_context(tc.psum_pool(name="psum", bufs=8))
 
-        idx = keep.tile([P, S // 16], U16)
-        idx2 = keep.tile([P, S2 // 16], U16)
-        words = [keep.tile([P, T], I32, name=f"words{a}", tag=f"words{a}", align_bytes=64) for a in range(3)]
+        idx = keep.tile([P, S // LIST], U16)
+        idx2 = keep.tile([P, S2 // LIST], U16)
+        text_words = [keep.tile([P, T], I32, name=f"words{a}", tag=f"words{a}", align_bytes=64) for a in range(3)]
         w1_raw = keep.tile([P, 4, H], F32, align_bytes=64)
-        planes = keep.tile([P, T // 4], I32, align_bytes=64)
-        plane2 = keep.tile([P, T2 // 4], I32, align_bytes=64)
+        text_planes = keep.tile([P, T // 4], I32, align_bytes=64)
         w4_raw = keep.tile([P, 2, H // 2], I32, align_bytes=64)
-        w4s_raw = keep.tile([P, 2, H // 4], I32, align_bytes=64, tag="w4s_then_words2")
+        w4_scales_raw = keep.tile([P, 2, H // 4], I32, align_bytes=64, tag="doc_words")
         gain = keep.tile([P, 2, 2], F32)
-        prior_rows = keep.tile([P, 32], F32, align_bytes=64)
-        prior_turned = keep.tile([P, 32], F32, align_bytes=64)
+        prior_rows = keep.tile([P, QUAD], F32, align_bytes=64)
+        prior_turned = keep.tile([P, QUAD], F32, align_bytes=64)
         prior_cols = keep.tile([P, S2 // P], F32)
-        v_planes = keep.tile([P, 2, S // 4], I32, align_bytes=64)
+        body_planes = keep.tile([P, 2, S // 4], I32, align_bytes=64)
         warm = keep.tile([P, 2], F32)
 
         nc.vector.memset(warm[:, 0:1], 0.0)
-        nc.gpsimd.memset(w4s_raw[:], 0)
+        nc.gpsimd.memset(w4_scales_raw[:], 0)
         for q in range(4):
-            nc.vector.memset(planes[32 * q : 32 * q + 12, :], 0)
-        nc.vector.memset(v_planes[96:P], 0)
-        nc.gpsimd.memset(plane2[:], 0)
-        for r in range(4):
-            nc.gpsimd.dma_start(plane2[r:P:32, :], tab2_scales[0, r:16:4, :].bitcast(I32))
+            nc.vector.memset(text_planes[QUAD * q : QUAD * q + FIRST_ROW, :], 0)
+        nc.gpsimd.memset(body_planes[3 * QUAD : P], 0)
 
-        def load_words(a):
-            nc.sync.dma_start(words[a][:], tab_words[a].rearrange("p t i -> p (t i)").bitcast(I32))
+        def load_text_words(a):
+            nc.sync.dma_start(text_words[a][:], tab_words[a].rearrange("p t i -> p (t i)").bitcast(I32))
 
         scale_rows = tab_scales.rearrange("a (h e r) n -> e (a h) r n", h=2, e=2)
 
-        def load_planes(queue, q):
-            queue.dma_start(planes[32 * q + 12 : 32 * q + 32, :], scale_rows[q % 2, q // 2 : q // 2 + 5].bitcast(I32))
+        def load_text_planes(queue, q):
+            queue.dma_start(
+                text_planes[QUAD * q + FIRST_ROW : QUAD * (q + 1), :], scale_rows[q % 2, q // 2 : q // 2 + 5].bitcast(I32)
+            )
 
         nc.sync.dma_start(idx[:], offs)
-        load_words(1)
-        load_planes(nc.scalar, 0)
-        load_planes(nc.sync, 1)
-        load_planes(nc.scalar, 2)
-        load_planes(nc.sync, 3)
+        load_text_words(1)
+        for q in range(4):
+            load_text_planes(nc.sync if q % 2 else nc.scalar, q)
         nc.sync.dma_start(w4_raw[:], w4_words.rearrange("a p n -> p a n").bitcast(I32))
-        load_words(2)
+        load_text_words(2)
         for r in range(4):
-            nc.sync.dma_start(w4s_raw[r:P:32], w4_scales[:, r:16:4, :].rearrange("a q n -> q a n").bitcast(I32))
+            nc.sync.dma_start(w4_scales_raw[r:P:QUAD], w4_scales[:, r:16:4, :].rearrange("a q n -> q a n").bitcast(I32))
         nc.sync.dma_start(w1_raw[:], w1.rearrange("(p j) c -> p j c", j=4))
-        load_words(0)
+        load_text_words(0)
         nc.sync.dma_start(idx2[:], offs2)
         nc.sync.dma_start(gain[:], g.rearrange("(p u e) -> p u e", u=2, e=2))
-        nc.sync.dma_start(prior_rows[:], prior.rearrange("(r b) -> r b", b=32).unsqueeze(0).to_broadcast([4, 32, 32]))
+        nc.sync.dma_start(
+            prior_rows[:], prior.rearrange("(r b) -> r b", b=QUAD).unsqueeze(0).to_broadcast([4, QUAD, QUAD])
+        )
         nc.scalar.activation(warm[:, 1:2], warm[:, 0:1], ACT.Ln, bias=1.0)
 
-        v_scales = keep.tile([P, S], U8, align_bytes=64)
-        v_codes = {
-            (a, half): keep.tile([P, HALF], U32, name=f"v_codes{a}{half}", tag=f"v_codes{a}{half}", align_bytes=64)
+        query_planes = keep.tile([P, S], U8, align_bytes=64)
+        query_codes = {
+            (a, half): keep.tile([P, HALF], U32, name=f"codes{a}{half}", tag=f"codes{a}{half}", align_bytes=64)
             for a in range(3)
             for half in range(2)
             if (a, half) != (0, 1)
@@ -91,37 +97,43 @@ def tile_list_sparse_lexical_scores_kernel(
             return slice(half * HALF, (half + 1) * HALF)
 
         def list_cols(half):
-            return slice(half * HALF // 16, (half + 1) * HALF // 16)
+            return slice(half * HALF // LIST, (half + 1) * HALF // LIST)
 
-        def gather_words(a, half):
-            nc.vector.tensor_copy(v_codes[a, half][:], words[a][:].bitcast(U32).indirect(idx[:, list_cols(half)]))
+        def gather_query_words(a, half):
+            window = text_words[a][:].bitcast(U32)
+            nc.vector.tensor_copy(query_codes[a, half][:], window.indirect(idx[:, list_cols(half)]))
 
         def gather_doc_scales(half):
-            nc.vector.tensor_copy(v2_scales[:, cols(half)], plane2[:].bitcast(U8).indirect(idx2[:, list_cols(half)]))
+            window = doc_plane[:].bitcast(U8)
+            nc.vector.tensor_copy(cand_scales[:, cols(half)], window.indirect(idx2[:, list_cols(half)]))
 
         def gather_doc_words(half):
-            nc.vector.tensor_copy(v2_codes[:, cols(half)], words2[:].bitcast(U32).indirect(idx2[:, list_cols(half)]))
+            window = doc_words[:].bitcast(U32)
+            nc.vector.tensor_copy(cand_codes[:, cols(half)], window.indirect(idx2[:, list_cols(half)]))
 
-        gather_words(1, 0)
-        nc.vector.tensor_copy(v_scales[:], planes[:].bitcast(U8).indirect(idx[:]))
+        gather_query_words(1, 0)
+        nc.vector.tensor_copy(query_planes[:], text_planes[:].bitcast(U8).indirect(idx[:]))
         for a in (1, 2):
-            nc.scalar.dma_start(v_planes[0:100, a - 1, :], v_scales[8 * a + 12 : 8 * a + 112, :].bitcast(I32))
-        gather_words(2, 0)
+            first = FIRST_ROW + PASS_ROWS * a
+            nc.scalar.dma_start(
+                body_planes[0:PLANE_ROWS, a - 1, :], query_planes[first : first + PLANE_ROWS, :].bitcast(I32)
+            )
+        gather_query_words(2, 0)
 
         w4_codes = keep.tile([P, 2, 2 * H], U8, align_bytes=64)
         w4_planes = keep.tile([P, 2, H], U8, align_bytes=64)
         nc.vector.tensor_copy(
             w4_planes[:].rearrange("p a (t m) -> p a t m", t=4),
-            w4s_raw[:].bitcast(U8).rearrange("p a (m t) -> p a t m", t=4),
+            w4_scales_raw[:].bitcast(U8).rearrange("p a (m t) -> p a t m", t=4),
         )
-        words2 = keep.tile([P, T2], I32, align_bytes=64, tag="w4s_then_words2")
-        nc.sync.dma_start(words2[:], tab2_words[0].rearrange("p t i -> p (t i)").bitcast(I32))
+        doc_words = keep.tile([P, T2], I32, align_bytes=64, tag="doc_words")
+        nc.sync.dma_start(doc_words[:], tab2_words[0].rearrange("p t i -> p (t i)").bitcast(I32))
         nc.vector.tensor_copy(
             w4_codes[:].bitcast(U16).rearrange("p a (t m) -> p a t m", t=4),
             w4_raw[:].bitcast(U16).rearrange("p a (m t) -> p a t m", t=4),
         )
 
-        w1_bf = keep.tile([P, 4 * H], BF16, tag="w1_bf_then_v2_codes", align_bytes=64)
+        w1_bf = keep.tile([P, 4 * H], BF16, align_bytes=64)
         w1_codes = keep.tile([P, H], U32, align_bytes=64)
         w1_plane = keep.tile([P, H], U8, align_bytes=64)
         for u in range(2):
@@ -137,9 +149,9 @@ def tile_list_sparse_lexical_scores_kernel(
                 out=w1_codes[:, at].bitcast(FP8X4), scales=w1_plane[:, at], in_=w1_bf[:, 8 * P * u : 8 * P * (u + 1)]
             )
 
-        gather_words(1, 1)
+        gather_query_words(1, 1)
         quantize_w1(0)
-        gather_words(0, 0)
+        gather_query_words(0, 0)
         quantize_w1(1)
 
         def logits(half, order):
@@ -149,21 +161,24 @@ def tile_list_sparse_lexical_scores_kernel(
                     if a == 0:
                         weights = w1_codes[:, P * t : P * (t + 1)].bitcast(FP8X4)
                         weight_scales = w1_plane[:, P * t : P * (t + 1)]
+                        plane = query_planes[FIRST_ROW:P]
                     else:
                         weights = w4_codes[:, a - 1, 2 * P * t : 2 * P * (t + 1)].bitcast(FP4X4)
                         weight_scales = w4_planes[:, a - 1, P * t : P * (t + 1)]
+                        plane = body_planes[:, a - 1, :].bitcast(U8)
                     nc.tensor.matmul_mx(
                         out=banks[t][:],
                         lhsT=weights,
                         lhsT_scale=weight_scales,
-                        rhs=v_codes[a, half][:].bitcast(FP8X4),
-                        rhs_scale=(v_planes[:, a - 1, :].bitcast(U8) if a else v_scales[12:P])[:, cols(half)],
+                        rhs=query_codes[a, half][:].bitcast(FP8X4),
+                        rhs_scale=plane[:, cols(half)],
                         start=(a == order[0]),
                         stop=(a == order[-1]),
                     )
             return banks
 
-        h_scales = keep.tile([P, S], U8, align_bytes=64)
+        h_codes = keep.tile([P, S], U32, align_bytes=64)
+        h_plane = keep.tile([P, S], U8, align_bytes=64)
 
         def term_weights(c, banks):
             inside = slice(c % 2 * CHUNK, (c % 2 + 1) * CHUNK)
@@ -172,8 +187,10 @@ def tile_list_sparse_lexical_scores_kernel(
                 nc.scalar.activation(pos[:, t // 2, t % 2, :], banks[t][:, inside], ACT.Relu)
             logs = work.tile([P, 2, CHUNK, 2], F32, name="logs")
             nc.scalar.activation(logs[:], pos[:].rearrange("p u e n -> p u n e"), ACT.Ln, bias=1.0)
-            h_bf = work.tile([P, CHUNK, 2, 2], BF16, name="h_bf", align_bytes=64)
-            nc.gpsimd.tensor_tensor(
+            h_bf = keep.tile(
+                [P, CHUNK, 2, 2], BF16, name=f"h_bf{c}", tag="codes10" if c else "doc_words", align_bytes=64
+            )
+            nc.vector.tensor_tensor(
                 h_bf[:],
                 logs[:].rearrange("p u n e -> p n u e"),
                 gain[:].unsqueeze(1).to_broadcast([P, CHUNK, 2, 2]),
@@ -182,53 +199,57 @@ def tile_list_sparse_lexical_scores_kernel(
             at = slice(c * CHUNK, (c + 1) * CHUNK)
             nc.vector.quantize_mx(
                 out=h_codes[:, at].bitcast(FP8X4),
-                scales=h_scales[:, at],
+                scales=h_plane[:, at],
                 in_=h_bf[:].rearrange("p n u e -> p (n u e)"),
             )
 
-        def scores(m0, count, at, on_vector):
-            width = HALF // count
-            bank = psum.tile([P, count, width], F32, tag="bank", name=f"score{m0}_{at.start}")
-            for i in range(count):
-                rows = slice((m0 + i) * P, (m0 + i + 1) * P)
-                nc.tensor.matmul_mx(
-                    out=bank[:, i, :],
-                    lhsT=v2_codes[:, rows].bitcast(FP8X4),
-                    lhsT_scale=v2_scales[:, rows],
-                    rhs=h_codes[:, at].bitcast(FP8X4),
-                    rhs_scale=h_scales[:, at],
-                    start=True,
-                    stop=True,
-                )
-            result = stage.tile([P, count, width], F32, name="result")
+        def scores(m, half, on_vector):
+            rows = slice(m * P, (m + 1) * P)
+            bank = psum.tile([P, HALF], F32, tag="bank", name=f"score{m}{half}")
+            nc.tensor.matmul_mx(
+                out=bank[:],
+                lhsT=cand_codes[:, rows].bitcast(FP8X4),
+                lhsT_scale=cand_scales[:, rows],
+                rhs=h_codes[:, cols(half)].bitcast(FP8X4),
+                rhs_scale=h_plane[:, cols(half)],
+                start=True,
+                stop=True,
+            )
+            result = stage.tile([P, HALF], F32, name="result")
             if on_vector:
-                nc.vector.tensor_tensor(
-                    result[:], bank[:], prior_cols[:, m0 : m0 + count].unsqueeze(2).to_broadcast([P, count, width]), ALU.add
-                )
+                nc.vector.tensor_scalar(result[:], bank[:], prior_cols[:, m : m + 1], None, ALU.add)
             else:
-                for i in range(count):
-                    nc.scalar.activation(result[:, i, :], bank[:, i, :], ACT.Identity, bias=prior_cols[:, m0 + i : m0 + i + 1])
-            nc.sync.dma_start(out[m0 * P : (m0 + count) * P, at].rearrange("(i p) n -> p i n", p=P), result[:])
+                nc.scalar.activation(result[:], bank[:], ACT.Identity, bias=prior_cols[:, m : m + 1])
+            nc.sync.dma_start(out[rows, cols(half)], result[:])
 
-        def chunk(c):
-            return slice(c * CHUNK, (c + 1) * CHUNK)
+        first_banks = logits(0, (1, 2, 0))
 
-        banks0 = logits(0, (1, 2, 0))
+        doc_plane = keep.tile([P, T2 // 4], I32, align_bytes=64, tag="codes10")
+        nc.gpsimd.memset(doc_plane[:], 0)
+        for r in range(4):
+            nc.sync.dma_start(doc_plane[r:P:QUAD, :], tab2_scales[0, r:16:4, :].bitcast(I32))
+
         nc.vector.transpose(prior_turned[:], prior_rows[:])
         for q in range(4):
-            nc.vector.tensor_copy(prior_cols[32 * q : 32 * q + 32, :], prior_turned[32 * q : 32 * q + 32, q : 32 : 4])
-        gather_words(2, 1)
-        v_codes[0, 1] = keep.tile([P, HALF], U32, name="v_codes01", tag="v_codes20", align_bytes=64)
-        gather_words(0, 1)
-        banks1 = logits(1, (0, 1, 2))
-        v2_scales = keep.tile([P, S2], U8, tag="words0", align_bytes=64)
-        v2_codes = keep.tile([P, S2], U32, tag="w1_bf_then_v2_codes", align_bytes=64)
-        for half in range(2):
-            gather_doc_scales(half)
+            quadrant = slice(QUAD * q, QUAD * (q + 1))
+            nc.vector.tensor_copy(prior_cols[quadrant, :], prior_turned[quadrant, q:QUAD:4])
+
+        gather_query_words(2, 1)
+        query_codes[0, 1] = keep.tile([P, HALF], U32, name="codes01", tag="codes20", align_bytes=64)
+        gather_query_words(0, 1)
+        second_banks = logits(1, (0, 1, 2))
+
+        cand_scales = keep.tile([P, S2], U8, align_bytes=64)
+        cand_codes = keep.tile([P, S2], U32, tag="words0", align_bytes=64)
         for half in range(2):
             gather_doc_words(half)
-        h_codes = keep.tile([P, S], U32, tag="w4s_then_words2", align_bytes=64)
-        for c in range(4):
-            term_weights(c, (banks0, banks1)[c // 2])
-            for m0 in (0, 2, 4, 6):
-                scores(m0, 2, chunk(c), c < 2 or (c, m0) in ((3, 2), (3, 6)))
+        term_weights(0, first_banks)
+        for half in range(2):
+            gather_doc_scales(half)
+        term_weights(1, first_banks)
+        for m in range(S2 // P):
+            scores(m, 0, False)
+        term_weights(2, second_banks)
+        term_weights(3, second_banks)
+        for m in range(S2 // P):
+            scores(m, 1, m in VECTOR_TILES)

@@ -20,11 +20,11 @@ T, S = 2048, 1024
 T2, S2 = 4096, 1024
 HALF = 512
 CHUNK = 256
+GROUP = 128
 LIST = 16
-FIRST_ROW = 12
-PASS_ROWS = 8
+BODY2_ROW, TITLE_ROW = 4, 8
+DOC_ROW = 12
 PLANE_ROWS = 3 * QUAD + 4
-VECTOR_TILES = (0, 1, 2, 4, 6)
 FLOPS = 2 * K * H * S + 2 * H * S2 * S
 
 
@@ -34,64 +34,66 @@ def tile_list_sparse_lexical_scores_kernel(
     nc = tc.nc
     with ExitStack() as ctx:
         keep = ctx.enter_context(tc.tile_pool(name="keep", bufs=1))
-        work = ctx.enter_context(tc.tile_pool(name="work", bufs=S // CHUNK))
-        stage = ctx.enter_context(tc.tile_pool(name="stage", bufs=S2 // P))
+        work = ctx.enter_context(tc.tile_pool(name="work", bufs=2))
+        stage = ctx.enter_context(tc.tile_pool(name="stage", bufs=8))
         psum = ctx.enter_context(tc.psum_pool(name="psum", bufs=8))
 
         idx = keep.tile([P, S // LIST], U16)
         idx2 = keep.tile([P, S2 // LIST], U16)
         text_words = [keep.tile([P, T], I32, name=f"words{a}", tag=f"words{a}", align_bytes=64) for a in range(3)]
         w1_raw = keep.tile([P, 4, H], F32, align_bytes=64)
-        text_planes = keep.tile([P, T // 4], I32, align_bytes=64)
+        text_planes = keep.tile([P, T // 4], I32, align_bytes=64, tag="text_planes")
+        doc_plane = keep.tile([P, T2 // 4], I32, align_bytes=64)
         w4_raw = keep.tile([P, 2, H // 2], I32, align_bytes=64)
-        w4_scales_raw = keep.tile([P, 2, H // 4], I32, align_bytes=64, tag="doc_words")
-        gain = keep.tile([P, 2, 2], F32)
+        w4_scales_raw = keep.tile([P, 2, H // 4], I32, align_bytes=64)
+        gain = keep.tile([P, 4], F32)
         prior_rows = keep.tile([P, QUAD], F32, align_bytes=64)
         prior_turned = keep.tile([P, QUAD], F32, align_bytes=64)
         prior_cols = keep.tile([P, S2 // P], F32)
-        body_planes = keep.tile([P, 2, S // 4], I32, align_bytes=64)
+        body2_plane = keep.tile([P, S // 4], I32, align_bytes=64)
         warm = keep.tile([P, 2], F32)
 
+        nc.gpsimd.dma_start(
+            prior_rows[:], prior.rearrange("(r b) -> r b", b=QUAD).unsqueeze(0).to_broadcast([4, QUAD, QUAD])
+        )
+        nc.vector.memset(w4_scales_raw[:], 0)
+        nc.vector.memset(text_planes[:], 0)
         nc.vector.memset(warm[:, 0:1], 0.0)
-        nc.gpsimd.memset(w4_scales_raw[:], 0)
-        for q in range(4):
-            nc.vector.memset(text_planes[QUAD * q : QUAD * q + FIRST_ROW, :], 0)
-        nc.gpsimd.memset(body_planes[3 * QUAD : P], 0)
+        nc.vector.memset(doc_plane[:], 0)
+        nc.vector.memset(body2_plane[3 * QUAD : P], 0)
 
         def load_text_words(a):
             nc.sync.dma_start(text_words[a][:], tab_words[a].rearrange("p t i -> p (t i)").bitcast(I32))
 
-        scale_rows = tab_scales.rearrange("a (h e r) n -> e (a h) r n", h=2, e=2)
+        def load_body_scales(queue, q):
+            queue.dma_start(text_planes[QUAD * q : QUAD * q + 8, :], tab_scales[1:3, 4 * q : 4 * q + 4, :].bitcast(I32))
 
-        def load_text_planes(queue, q):
-            queue.dma_start(
-                text_planes[QUAD * q + FIRST_ROW : QUAD * (q + 1), :], scale_rows[q % 2, q // 2 : q // 2 + 5].bitcast(I32)
-            )
+        def load_title_scales(queue, r):
+            queue.dma_start(text_planes[TITLE_ROW + r : P : QUAD, :], tab_scales[0, r:16:4, :].bitcast(I32))
 
-        nc.sync.dma_start(idx[:], offs)
-        load_text_words(1)
         for q in range(4):
-            load_text_planes(nc.sync if q % 2 else nc.scalar, q)
-        nc.sync.dma_start(w4_raw[:], w4_words.rearrange("a p n -> p a n").bitcast(I32))
-        load_text_words(2)
+            load_body_scales(nc.gpsimd, q)
         for r in range(4):
-            nc.sync.dma_start(w4_scales_raw[r:P:QUAD], w4_scales[:, r:16:4, :].rearrange("a q n -> q a n").bitcast(I32))
-        nc.sync.dma_start(w1_raw[:], w1.rearrange("(p j) c -> p j c", j=4))
-        load_text_words(0)
+            nc.gpsimd.dma_start(doc_plane[DOC_ROW + r : P : QUAD, :], tab2_scales[0, r:16:4, :].bitcast(I32))
+        nc.scalar.dma_start(w4_raw[:], w4_words.rearrange("a p n -> p a n").bitcast(I32))
+        for r in range(4):
+            nc.scalar.dma_start(w4_scales_raw[r:P:QUAD], w4_scales[:, r:16:4, :].rearrange("a q n -> q a n").bitcast(I32))
+        nc.sync.dma_start(idx[:], offs)
         nc.sync.dma_start(idx2[:], offs2)
-        nc.sync.dma_start(gain[:], g.rearrange("(p u e) -> p u e", u=2, e=2))
-        nc.sync.dma_start(
-            prior_rows[:], prior.rearrange("(r b) -> r b", b=QUAD).unsqueeze(0).to_broadcast([4, QUAD, QUAD])
-        )
+        load_text_words(1)
+        load_title_scales(nc.sync, 0)
+        nc.sync.dma_start(w1_raw[:], w1.rearrange("(p j) c -> p j c", j=4))
+        for r in range(1, 4):
+            load_title_scales(nc.sync, r)
+        load_text_words(2)
+        load_text_words(0)
+        nc.sync.dma_start(gain[:], g.rearrange("(p t) -> p t", t=4))
         nc.scalar.activation(warm[:, 1:2], warm[:, 0:1], ACT.Ln, bias=1.0)
 
         query_planes = keep.tile([P, S], U8, align_bytes=64)
-        query_codes = {
-            (a, half): keep.tile([P, HALF], U32, name=f"codes{a}{half}", tag=f"codes{a}{half}", align_bytes=64)
-            for a in range(3)
-            for half in range(2)
-            if (a, half) != (0, 1)
-        }
+        cand_codes = keep.tile([P, S2], U32, align_bytes=64)
+        query_codes = {}
+        cand_scales = {0: keep.tile([P, HALF], U8, name="cand_scales0", align_bytes=64, tag="text_planes")}
 
         def cols(half):
             return slice(half * HALF, (half + 1) * HALF)
@@ -99,42 +101,42 @@ def tile_list_sparse_lexical_scores_kernel(
         def list_cols(half):
             return slice(half * HALF // LIST, (half + 1) * HALF // LIST)
 
-        def gather_query_words(a, half):
-            window = text_words[a][:].bitcast(U32)
-            nc.vector.tensor_copy(query_codes[a, half][:], window.indirect(idx[:, list_cols(half)]))
+        def gather_query_words(a, half, codes):
+            query_codes[a, half] = codes
+            nc.vector.tensor_copy(codes, text_words[a][:].bitcast(U32).indirect(idx[:, list_cols(half)]))
 
         def gather_doc_scales(half):
             window = doc_plane[:].bitcast(U8)
-            nc.vector.tensor_copy(cand_scales[:, cols(half)], window.indirect(idx2[:, list_cols(half)]))
+            nc.vector.tensor_copy(cand_scales[half][:], window.indirect(idx2[:, list_cols(half)]))
 
         def gather_doc_words(half):
             window = doc_words[:].bitcast(U32)
             nc.vector.tensor_copy(cand_codes[:, cols(half)], window.indirect(idx2[:, list_cols(half)]))
 
-        gather_query_words(1, 0)
+        first_codes = keep.tile([P, 2, HALF], U32, align_bytes=64)
+        body1_second = keep.tile([P, HALF], U32, align_bytes=64)
+        body2_first = keep.tile([P, HALF], U32, align_bytes=64, tag="body2_codes")
+        gather_query_words(1, 0, first_codes[:, 1, :])
         nc.vector.tensor_copy(query_planes[:], text_planes[:].bitcast(U8).indirect(idx[:]))
-        for a in (1, 2):
-            first = FIRST_ROW + PASS_ROWS * a
-            nc.scalar.dma_start(
-                body_planes[0:PLANE_ROWS, a - 1, :], query_planes[first : first + PLANE_ROWS, :].bitcast(I32)
-            )
-        gather_query_words(2, 0)
+        nc.scalar.dma_start(
+            body2_plane[0:PLANE_ROWS, :], query_planes[BODY2_ROW : BODY2_ROW + PLANE_ROWS, :].bitcast(I32)
+        )
+        gather_query_words(1, 1, body1_second[:])
+        gather_query_words(2, 0, body2_first[:])
 
         w4_codes = keep.tile([P, 2, 2 * H], U8, align_bytes=64)
         w4_planes = keep.tile([P, 2, H], U8, align_bytes=64)
         nc.vector.tensor_copy(
-            w4_planes[:].rearrange("p a (t m) -> p a t m", t=4),
-            w4_scales_raw[:].bitcast(U8).rearrange("p a (m t) -> p a t m", t=4),
-        )
-        doc_words = keep.tile([P, T2], I32, align_bytes=64, tag="doc_words")
-        nc.sync.dma_start(doc_words[:], tab2_words[0].rearrange("p t i -> p (t i)").bitcast(I32))
-        nc.vector.tensor_copy(
             w4_codes[:].bitcast(U16).rearrange("p a (t m) -> p a t m", t=4),
             w4_raw[:].bitcast(U16).rearrange("p a (m t) -> p a t m", t=4),
         )
+        nc.vector.tensor_copy(
+            w4_planes[:].rearrange("p a (t m) -> p a t m", t=4),
+            w4_scales_raw[:].bitcast(U8).rearrange("p a (m t) -> p a t m", t=4),
+        )
 
-        w1_bf = keep.tile([P, 4 * H], BF16, align_bytes=64)
-        w1_codes = keep.tile([P, H], U32, align_bytes=64)
+        w1_bf = keep.tile([P, 4 * H], BF16, align_bytes=64, tag="doc_words")
+        w1_codes = keep.tile([P, H], U32, align_bytes=64, tag="w1_codes")
         w1_plane = keep.tile([P, H], U8, align_bytes=64)
         for u in range(2):
             nc.scalar.activation(
@@ -143,113 +145,118 @@ def tile_list_sparse_lexical_scores_kernel(
                 ACT.Identity,
             )
 
-        def quantize_w1(u):
-            at = slice(2 * P * u, 2 * P * (u + 1))
-            nc.vector.quantize_mx(
-                out=w1_codes[:, at].bitcast(FP8X4), scales=w1_plane[:, at], in_=w1_bf[:, 8 * P * u : 8 * P * (u + 1)]
-            )
 
-        gather_query_words(1, 1)
-        quantize_w1(0)
-        gather_query_words(0, 0)
-        quantize_w1(1)
+        nc.vector.quantize_mx(out=w1_codes[:].bitcast(FP8X4), scales=w1_plane[:], in_=w1_bf[:])
+        doc_words = keep.tile([P, T2], I32, align_bytes=64, tag="doc_words")
+        nc.sync.dma_start(doc_words[:], tab2_words[0].rearrange("p t i -> p (t i)").bitcast(I32))
+        gather_query_words(0, 0, first_codes[:, 0, :])
 
-        def logits(half, order):
-            banks = [psum.tile([P, HALF], F32, tag="bank", name=f"logit{half}{t}") for t in range(4)]
-            for a in order:
+        banks = {}
+
+        def logits(half):
+            groups = range(half * HALF // GROUP, (half + 1) * HALF // GROUP)
+            for c in groups:
+                banks[c] = psum.tile([P, 4, GROUP], F32, tag="bank", name=f"logit{c}")
+            for c, a in [(c, 1) for c in groups] + [(c, a) for c in groups for a in (0, 2)]:
+                plane = (query_planes[TITLE_ROW:P], query_planes[:], body2_plane[:].bitcast(U8))[a]
+                inside = slice(c * GROUP % HALF, c * GROUP % HALF + GROUP)
                 for t in range(4):
                     if a == 0:
                         weights = w1_codes[:, P * t : P * (t + 1)].bitcast(FP8X4)
                         weight_scales = w1_plane[:, P * t : P * (t + 1)]
-                        plane = query_planes[FIRST_ROW:P]
                     else:
                         weights = w4_codes[:, a - 1, 2 * P * t : 2 * P * (t + 1)].bitcast(FP4X4)
                         weight_scales = w4_planes[:, a - 1, P * t : P * (t + 1)]
-                        plane = body_planes[:, a - 1, :].bitcast(U8)
                     nc.tensor.matmul_mx(
-                        out=banks[t][:],
+                        out=banks[c][:, t, :],
                         lhsT=weights,
                         lhsT_scale=weight_scales,
-                        rhs=query_codes[a, half][:].bitcast(FP8X4),
-                        rhs_scale=plane[:, cols(half)],
-                        start=(a == order[0]),
-                        stop=(a == order[-1]),
+                        rhs=query_codes[a, half][:, inside].bitcast(FP8X4),
+                        rhs_scale=plane[:, c * GROUP : (c + 1) * GROUP],
+                        start=(a == 1 and t == 0),
+                        stop=(a == 2 and t == 3),
                     )
-            return banks
 
         h_codes = keep.tile([P, S], U32, align_bytes=64)
         h_plane = keep.tile([P, S], U8, align_bytes=64)
+        logs = {}
 
-        def term_weights(c, banks):
-            inside = slice(c % 2 * CHUNK, (c % 2 + 1) * CHUNK)
-            pos = work.tile([P, 2, 2, CHUNK], F32, name="pos", bufs=1)
-            for t in range(4):
-                nc.scalar.activation(pos[:, t // 2, t % 2, :], banks[t][:, inside], ACT.Relu)
-            logs = work.tile([P, 2, CHUNK, 2], F32, name="logs")
-            nc.scalar.activation(logs[:], pos[:].rearrange("p u e n -> p u n e"), ACT.Ln, bias=1.0)
-            h_bf = keep.tile(
-                [P, CHUNK, 2, 2], BF16, name=f"h_bf{c}", tag="codes10" if c else "doc_words", align_bytes=64
-            )
-            nc.vector.tensor_tensor(
-                h_bf[:],
-                logs[:].rearrange("p u n e -> p n u e"),
-                gain[:].unsqueeze(1).to_broadcast([P, CHUNK, 2, 2]),
-                ALU.mult,
-            )
+        def saturate(c):
+            pos = work.tile([P, CHUNK, 4], F32, name="pos")
+            for e in range(CHUNK // GROUP):
+                nc.scalar.activation(
+                    pos[:, e * GROUP : (e + 1) * GROUP, :],
+                    banks[c * CHUNK // GROUP + e][:].rearrange("p t n -> p n t"),
+                    ACT.Relu,
+                )
+            logs[c] = work.tile([P, CHUNK, 4], F32, name="logs")
+            nc.scalar.activation(logs[c][:], pos[:], ACT.Ln, bias=1.0)
+
+        def quantize_h(c):
+            h_bf = keep.tile([P, CHUNK, 4], BF16, name=f"h_bf{c}", tag="doc_words" if c == 1 else f"h_bf{c}", align_bytes=64)
+            nc.vector.tensor_tensor(h_bf[:], logs[c][:], gain[:].unsqueeze(1).to_broadcast([P, CHUNK, 4]), ALU.mult)
             at = slice(c * CHUNK, (c + 1) * CHUNK)
             nc.vector.quantize_mx(
-                out=h_codes[:, at].bitcast(FP8X4),
-                scales=h_plane[:, at],
-                in_=h_bf[:].rearrange("p n u e -> p (n u e)"),
+                out=h_codes[:, at].bitcast(FP8X4), scales=h_plane[:, at], in_=h_bf[:].rearrange("p n t -> p (n t)")
             )
 
-        def scores(m, half, on_vector):
-            rows = slice(m * P, (m + 1) * P)
-            bank = psum.tile([P, HALF], F32, tag="bank", name=f"score{m}{half}")
-            nc.tensor.matmul_mx(
-                out=bank[:],
-                lhsT=cand_codes[:, rows].bitcast(FP8X4),
-                lhsT_scale=cand_scales[:, rows],
-                rhs=h_codes[:, cols(half)].bitcast(FP8X4),
-                rhs_scale=h_plane[:, cols(half)],
-                start=True,
-                stop=True,
-            )
-            result = stage.tile([P, HALF], F32, name="result")
+        def scores(c, pair, on_vector):
+            at = slice(c * CHUNK, (c + 1) * CHUNK)
+            bank = psum.tile([P, 2, CHUNK], F32, tag="bank", name=f"score{c}{pair}")
+            for e in range(2):
+                rows = slice((2 * pair + e) * P, (2 * pair + e + 1) * P)
+                nc.tensor.matmul_mx(
+                    out=bank[:, e, :],
+                    lhsT=cand_codes[:, rows].bitcast(FP8X4),
+                    lhsT_scale=cand_scales[pair // 2][DOC_ROW:P, rows.start % HALF : rows.start % HALF + P],
+                    rhs=h_codes[:, at].bitcast(FP8X4),
+                    rhs_scale=h_plane[:, at],
+                    start=True,
+                    stop=True,
+                )
+            result = stage.tile([P, 2, CHUNK], F32, name="result")
             if on_vector:
-                nc.vector.tensor_scalar(result[:], bank[:], prior_cols[:, m : m + 1], None, ALU.add)
+                priors = prior_cols[:, 2 * pair : 2 * pair + 2].unsqueeze(2).to_broadcast([P, 2, CHUNK])
+                nc.vector.tensor_tensor(result[:], bank[:], priors, ALU.add)
             else:
-                nc.scalar.activation(result[:], bank[:], ACT.Identity, bias=prior_cols[:, m : m + 1])
-            nc.sync.dma_start(out[rows, cols(half)], result[:])
+                for e in range(2):
+                    m = 2 * pair + e
+                    nc.scalar.activation(result[:, e, :], bank[:, e, :], ACT.Identity, bias=prior_cols[:, m : m + 1])
+            rows = out[2 * pair * P : 2 * (pair + 1) * P, at]
+            nc.sync.dma_start(rows.rearrange("(e p) n -> p e n", e=2), result[:])
 
-        first_banks = logits(0, (1, 2, 0))
+        logits(0)
 
-        doc_plane = keep.tile([P, T2 // 4], I32, align_bytes=64, tag="codes10")
-        nc.gpsimd.memset(doc_plane[:], 0)
-        for r in range(4):
-            nc.sync.dma_start(doc_plane[r:P:QUAD, :], tab2_scales[0, r:16:4, :].bitcast(I32))
+        title_second = keep.tile([P, HALF], U32, align_bytes=64)
+        gather_query_words(0, 1, title_second[:])
+        cand_scales[1] = keep.tile([P, HALF], U8, name="cand_scales1", align_bytes=64, tag="words0")
+        gather_doc_scales(0)
+        body2_second = keep.tile([P, HALF], U32, align_bytes=64, tag="body2_codes")
+        gather_query_words(2, 1, body2_second[:])
+        logits(1)
 
         nc.vector.transpose(prior_turned[:], prior_rows[:])
         for q in range(4):
             quadrant = slice(QUAD * q, QUAD * (q + 1))
             nc.vector.tensor_copy(prior_cols[quadrant, :], prior_turned[quadrant, q:QUAD:4])
 
-        gather_query_words(2, 1)
-        query_codes[0, 1] = keep.tile([P, HALF], U32, name="codes01", tag="codes20", align_bytes=64)
-        gather_query_words(0, 1)
-        second_banks = logits(1, (0, 1, 2))
-
-        cand_scales = keep.tile([P, S2], U8, align_bytes=64)
-        cand_codes = keep.tile([P, S2], U32, tag="words0", align_bytes=64)
-        for half in range(2):
-            gather_doc_words(half)
-        term_weights(0, first_banks)
-        for half in range(2):
-            gather_doc_scales(half)
-        term_weights(1, first_banks)
-        for m in range(S2 // P):
-            scores(m, 0, False)
-        term_weights(2, second_banks)
-        term_weights(3, second_banks)
-        for m in range(S2 // P):
-            scores(m, 1, m in VECTOR_TILES)
+        gather_doc_scales(1)
+        saturate(0)
+        gather_doc_words(0)
+        quantize_h(0)
+        gather_doc_words(1)
+        saturate(1)
+        quantize_h(1)
+        scores(0, 0, False)
+        scores(0, 1, False)
+        saturate(2)
+        quantize_h(2)
+        saturate(3)
+        quantize_h(3)
+        scores(0, 2, True)
+        scores(0, 3, True)
+        for pair in range(4):
+            scores(1, pair, False)
+        for c in (2, 3):
+            for pair in range(4):
+                scores(c, pair, pair % 2 == 0)

@@ -53,10 +53,7 @@ def tile_list_sparse_lexical_scores_kernel(
         body2_plane = keep.tile([P, S // 4], I32, align_bytes=64)
         warm = keep.tile([P, 2], F32)
 
-        nc.gpsimd.dma_start(
-            prior_rows[:], prior.rearrange("(r b) -> r b", b=QUAD).unsqueeze(0).to_broadcast([4, QUAD, QUAD])
-        )
-        nc.vector.memset(w4_scales_raw[:], 0)
+        nc.gpsimd.memset(w4_scales_raw[:], 0)
         nc.vector.memset(text_planes[:], 0)
         nc.vector.memset(warm[:, 0:1], 0.0)
         nc.vector.memset(doc_plane[:], 0)
@@ -71,21 +68,23 @@ def tile_list_sparse_lexical_scores_kernel(
         def load_title_scales(queue, r):
             queue.dma_start(text_planes[TITLE_ROW + r : P : QUAD, :], tab_scales[0, r:16:4, :].bitcast(I32))
 
-        for q in range(4):
-            load_body_scales(nc.gpsimd, q)
-        for r in range(4):
-            nc.gpsimd.dma_start(doc_plane[DOC_ROW + r : P : QUAD, :], tab2_scales[0, r:16:4, :].bitcast(I32))
         nc.scalar.dma_start(w4_raw[:], w4_words.rearrange("a p n -> p a n").bitcast(I32))
         for r in range(4):
             nc.scalar.dma_start(w4_scales_raw[r:P:QUAD], w4_scales[:, r:16:4, :].rearrange("a q n -> q a n").bitcast(I32))
         nc.sync.dma_start(idx[:], offs)
+        nc.sync.dma_start(
+            prior_rows[:], prior.rearrange("(r b) -> r b", b=QUAD).unsqueeze(0).to_broadcast([4, QUAD, QUAD])
+        )
         nc.sync.dma_start(idx2[:], offs2)
         load_text_words(1)
-        load_title_scales(nc.sync, 0)
+        for q in range(4):
+            load_body_scales(nc.sync, q)
         nc.sync.dma_start(w1_raw[:], w1.rearrange("(p j) c -> p j c", j=4))
-        for r in range(1, 4):
+        for r in range(4):
             load_title_scales(nc.sync, r)
         load_text_words(2)
+        for r in range(4):
+            nc.sync.dma_start(doc_plane[DOC_ROW + r : P : QUAD, :], tab2_scales[0, r:16:4, :].bitcast(I32))
         load_text_words(0)
         nc.sync.dma_start(gain[:], g.rearrange("(p t) -> p t", t=4))
         nc.scalar.activation(warm[:, 1:2], warm[:, 0:1], ACT.Ln, bias=1.0)
@@ -93,7 +92,7 @@ def tile_list_sparse_lexical_scores_kernel(
         query_planes = keep.tile([P, S], U8, align_bytes=64)
         cand_codes = keep.tile([P, S2], U32, align_bytes=64)
         query_codes = {}
-        cand_scales = {0: keep.tile([P, HALF], U8, name="cand_scales0", align_bytes=64, tag="text_planes")}
+        cand_scales = {0: keep.tile([P, HALF], U8, name="cand_scales0", align_bytes=64)}
 
         def cols(half):
             return slice(half * HALF, (half + 1) * HALF)
@@ -136,7 +135,7 @@ def tile_list_sparse_lexical_scores_kernel(
         )
 
         w1_bf = keep.tile([P, 4 * H], BF16, align_bytes=64, tag="doc_words")
-        w1_codes = keep.tile([P, H], U32, align_bytes=64, tag="w1_codes")
+        w1_codes = keep.tile([P, H], U32, align_bytes=64, tag="text_planes")
         w1_plane = keep.tile([P, H], U8, align_bytes=64)
         for u in range(2):
             nc.scalar.activation(

@@ -22,7 +22,7 @@ HALF = 512
 CHUNK = 256
 GROUP = 128
 LIST = 16
-BODY2_ROW, TITLE_ROW = 4, 8
+BODY2_ROW, TITLE_ROW = 16, 8
 DOC_ROW = 12
 PLANE_ROWS = 3 * QUAD + 4
 FLOPS = 2 * K * H * S + 2 * H * S2 * S
@@ -34,130 +34,134 @@ def tile_list_sparse_lexical_scores_kernel(
     nc = tc.nc
     with ExitStack() as ctx:
         keep = ctx.enter_context(tc.tile_pool(name="keep", bufs=1))
-        work = ctx.enter_context(tc.tile_pool(name="work", bufs=2))
         stage = ctx.enter_context(tc.tile_pool(name="stage", bufs=8))
-        psum = ctx.enter_context(tc.psum_pool(name="psum", bufs=8))
+        psum = ctx.enter_context(tc.psum_pool(name="psum", bufs=1))
 
         idx = keep.tile([P, S // LIST], U16)
         idx2 = keep.tile([P, S2 // LIST], U16)
         text_words = [keep.tile([P, T], I32, name=f"words{a}", tag=f"words{a}", align_bytes=64) for a in range(3)]
-        w1_raw = keep.tile([P, 4, H], F32, align_bytes=64)
+        w1_raw = keep.tile([P, 4, H], F32, align_bytes=64, tag="w1_raw")
         text_planes = keep.tile([P, T // 4], I32, align_bytes=64, tag="text_planes")
-        doc_plane = keep.tile([P, T2 // 4], I32, align_bytes=64)
+        doc_rows = keep.tile([P, T2 // 4], I32, align_bytes=64)
+        cand_plane = keep.tile([P, S2 // 4], I32, align_bytes=64)
+        doc_words = keep.tile([P, T2], I32, align_bytes=64)
         w4_raw = keep.tile([P, 2, H // 2], I32, align_bytes=64)
         w4_scales_raw = keep.tile([P, 2, H // 4], I32, align_bytes=64)
         gain = keep.tile([P, 4], F32)
         prior_rows = keep.tile([P, QUAD], F32, align_bytes=64)
         prior_turned = keep.tile([P, QUAD], F32, align_bytes=64)
         prior_cols = keep.tile([P, S2 // P], F32)
-        body2_plane = keep.tile([P, S // 4], I32, align_bytes=64)
+        body_planes = keep.tile([P, 2, S // 4], I32, align_bytes=64)
         warm = keep.tile([P, 2], F32)
 
-        nc.gpsimd.memset(w4_scales_raw[:], 0)
+        nc.vector.memset(doc_rows[:], 0)
         nc.vector.memset(text_planes[:], 0)
         nc.vector.memset(warm[:, 0:1], 0.0)
-        nc.vector.memset(doc_plane[:], 0)
-        nc.vector.memset(body2_plane[3 * QUAD : P], 0)
+        nc.vector.memset(w4_scales_raw[:], 0)
+        nc.vector.memset(cand_plane[:], 0)
+        nc.vector.memset(body_planes[3 * QUAD : P], 0)
 
         def load_text_words(a):
             nc.sync.dma_start(text_words[a][:], tab_words[a].rearrange("p t i -> p (t i)").bitcast(I32))
 
         def load_body_scales(queue, q):
-            queue.dma_start(text_planes[QUAD * q : QUAD * q + 8, :], tab_scales[1:3, 4 * q : 4 * q + 4, :].bitcast(I32))
+            rows = tab_scales[1:3, q:16:4, :].rearrange("a q n -> q a n")
+            queue.dma_start(text_planes[q:P:BODY2_ROW, :], rows.bitcast(I32))
 
         def load_title_scales(queue, r):
-            queue.dma_start(text_planes[TITLE_ROW + r : P : QUAD, :], tab_scales[0, r:16:4, :].bitcast(I32))
+            queue.dma_start(text_planes[QUAD * r : QUAD * r + 12, :], tab_scales[:, 4 * r : 4 * r + 4, :].bitcast(I32))
 
-        nc.scalar.dma_start(w4_raw[:], w4_words.rearrange("a p n -> p a n").bitcast(I32))
-        for r in range(4):
-            nc.scalar.dma_start(w4_scales_raw[r:P:QUAD], w4_scales[:, r:16:4, :].rearrange("a q n -> q a n").bitcast(I32))
+        nc.sync.dma_start(idx2[:], offs2)
         nc.sync.dma_start(idx[:], offs)
-        nc.sync.dma_start(
+        nc.sync.dma_start(w1_raw[:], w1.rearrange("(p j) c -> p j c", j=4))
+        load_title_scales(nc.sync, 0)
+        load_title_scales(nc.sync, 1)
+        load_text_words(0)
+        load_text_words(1)
+        nc.sync.dma_start(w4_scales_raw[0:P:QUAD], w4_scales[:, 0:16:4, :].rearrange("a q n -> q a n").bitcast(I32))
+        nc.sync.dma_start(w4_scales_raw[1:P:QUAD], w4_scales[:, 1:16:4, :].rearrange("a q n -> q a n").bitcast(I32))
+        nc.sync.dma_start(w4_scales_raw[2:P:QUAD], w4_scales[:, 2:16:4, :].rearrange("a q n -> q a n").bitcast(I32))
+        nc.sync.dma_start(w4_scales_raw[3:P:QUAD], w4_scales[:, 3:16:4, :].rearrange("a q n -> q a n").bitcast(I32))
+        load_text_words(2)
+        nc.scalar.dma_start(w4_raw[:], w4_words.rearrange("a p n -> p a n").bitcast(I32))
+        nc.scalar.dma_start(
             prior_rows[:], prior.rearrange("(r b) -> r b", b=QUAD).unsqueeze(0).to_broadcast([4, QUAD, QUAD])
         )
-        nc.sync.dma_start(idx2[:], offs2)
-        load_text_words(1)
-        for q in range(4):
-            load_body_scales(nc.sync, q)
-        nc.sync.dma_start(w1_raw[:], w1.rearrange("(p j) c -> p j c", j=4))
-        for r in range(4):
-            load_title_scales(nc.sync, r)
-        load_text_words(2)
-        for r in range(4):
-            nc.sync.dma_start(doc_plane[DOC_ROW + r : P : QUAD, :], tab2_scales[0, r:16:4, :].bitcast(I32))
-        load_text_words(0)
-        nc.sync.dma_start(gain[:], g.rearrange("(p t) -> p t", t=4))
+        nc.scalar.dma_start(doc_rows[0:P:8, :], tab2_scales[0].bitcast(I32))
+        load_title_scales(nc.scalar, 2)
+        load_title_scales(nc.scalar, 3)
+        nc.scalar.dma_start(gain[:], g.rearrange("(p t) -> p t", t=4))
         nc.scalar.activation(warm[:, 1:2], warm[:, 0:1], ACT.Ln, bias=1.0)
 
         query_planes = keep.tile([P, S], U8, align_bytes=64)
-        cand_codes = keep.tile([P, S2], U32, align_bytes=64)
+        cand_codes = {}
         query_codes = {}
-        cand_scales = {0: keep.tile([P, HALF], U8, name="cand_scales0", align_bytes=64)}
-
-        def cols(half):
-            return slice(half * HALF, (half + 1) * HALF)
+        cand_rows = keep.tile([P, S2], U8, align_bytes=64)
 
         def list_cols(half):
             return slice(half * HALF // LIST, (half + 1) * HALF // LIST)
 
-        def gather_query_words(a, half, codes):
+        def gather_query_words(a, half, tag, pieces=1):
+            codes = keep.tile([P, HALF], U32, name=f"codes{a}{half}", tag=tag, align_bytes=64)
             query_codes[a, half] = codes
-            nc.vector.tensor_copy(codes, text_words[a][:].bitcast(U32).indirect(idx[:, list_cols(half)]))
+            width = HALF // pieces
+            for first in range(0, HALF, width):
+                entries = slice((half * HALF + first) // LIST, (half * HALF + first + width) // LIST)
+                window = text_words[a][:].bitcast(U32)
+                nc.vector.tensor_copy(codes[:, first : first + width], window.indirect(idx[:, entries]))
 
-        def gather_doc_scales(half):
-            window = doc_plane[:].bitcast(U8)
-            nc.vector.tensor_copy(cand_scales[half][:], window.indirect(idx2[:, list_cols(half)]))
-
-        def gather_doc_words(half):
+        def gather_doc_words(half, tag):
+            cand_codes[half] = keep.tile([P, HALF], U32, name=f"cand_codes{half}", tag=tag, align_bytes=64)
             window = doc_words[:].bitcast(U32)
-            nc.vector.tensor_copy(cand_codes[:, cols(half)], window.indirect(idx2[:, list_cols(half)]))
+            nc.vector.tensor_copy(cand_codes[half][:], window.indirect(idx2[:, list_cols(half)]))
 
-        first_codes = keep.tile([P, 2, HALF], U32, align_bytes=64)
-        body1_second = keep.tile([P, HALF], U32, align_bytes=64)
-        body2_first = keep.tile([P, HALF], U32, align_bytes=64, tag="body2_codes")
-        gather_query_words(1, 0, first_codes[:, 1, :])
-        nc.vector.tensor_copy(query_planes[:], text_planes[:].bitcast(U8).indirect(idx[:]))
-        nc.scalar.dma_start(
-            body2_plane[0:PLANE_ROWS, :], query_planes[BODY2_ROW : BODY2_ROW + PLANE_ROWS, :].bitcast(I32)
-        )
-        gather_query_words(1, 1, body1_second[:])
-        gather_query_words(2, 0, body2_first[:])
+        def gather_query_scales():
+            nc.vector.tensor_copy(query_planes[:], text_planes[:].bitcast(U8).indirect(idx[:]))
+            for a in (1, 2):
+                nc.sync.dma_start(
+                    body_planes[0:PLANE_ROWS, a - 1, :], query_planes[4 * a : 4 * a + PLANE_ROWS, :].bitcast(I32)
+                )
 
         w4_codes = keep.tile([P, 2, 2 * H], U8, align_bytes=64)
         w4_planes = keep.tile([P, 2, H], U8, align_bytes=64)
-        nc.vector.tensor_copy(
-            w4_codes[:].bitcast(U16).rearrange("p a (t m) -> p a t m", t=4),
-            w4_raw[:].bitcast(U16).rearrange("p a (m t) -> p a t m", t=4),
-        )
-        nc.vector.tensor_copy(
-            w4_planes[:].rearrange("p a (t m) -> p a t m", t=4),
-            w4_scales_raw[:].bitcast(U8).rearrange("p a (m t) -> p a t m", t=4),
-        )
 
-        w1_bf = keep.tile([P, 4 * H], BF16, align_bytes=64, tag="doc_words")
-        w1_codes = keep.tile([P, H], U32, align_bytes=64, tag="text_planes")
-        w1_plane = keep.tile([P, H], U8, align_bytes=64)
-        for u in range(2):
-            nc.scalar.activation(
-                w1_bf[:].rearrange("p (t m j) -> p m j t", t=4, j=4)[:, :, :, 2 * u : 2 * u + 2],
-                w1_raw[:].rearrange("p j (m t) -> p m j t", t=4)[:, :, :, 2 * u : 2 * u + 2],
-                ACT.Identity,
+        def order_w4_words():
+            nc.vector.tensor_copy(
+                w4_codes[:].bitcast(U16).rearrange("p a (t m) -> p a t m", t=4),
+                w4_raw[:].bitcast(U16).rearrange("p a (m t) -> p a t m", t=4),
             )
 
+        def order_w4_scales():
+            nc.vector.tensor_copy(
+                w4_planes[:].rearrange("p a (t m) -> p a t m", t=4),
+                w4_scales_raw[:].bitcast(U8).rearrange("p a (m t) -> p a t m", t=4),
+            )
 
-        nc.vector.quantize_mx(out=w1_codes[:].bitcast(FP8X4), scales=w1_plane[:], in_=w1_bf[:])
-        doc_words = keep.tile([P, T2], I32, align_bytes=64, tag="doc_words")
-        nc.sync.dma_start(doc_words[:], tab2_words[0].rearrange("p t i -> p (t i)").bitcast(I32))
-        gather_query_words(0, 0, first_codes[:, 0, :])
+        w1_bf = keep.tile([P, 4 * H], BF16, align_bytes=64, tag="w1_bf")
+        w1_plane = keep.tile([P, H], U8, align_bytes=64)
+
+        def round_w1():
+            for u in range(2):
+                nc.scalar.activation(
+                    w1_bf[:].rearrange("p (t m j) -> p m j t", t=4, j=4)[:, :, :, 2 * u : 2 * u + 2],
+                    w1_raw[:].rearrange("p j (m t) -> p m j t", t=4)[:, :, :, 2 * u : 2 * u + 2],
+                    ACT.Identity,
+                )
+
+        def turn_prior():
+            nc.vector.transpose(prior_turned[:], prior_rows[:])
+            for q in range(4):
+                quadrant = slice(QUAD * q, QUAD * (q + 1))
+                nc.vector.tensor_copy(prior_cols[quadrant, :], prior_turned[quadrant, q:QUAD:4])
 
         banks = {}
 
-        def logits(half):
+        def logits(half, order):
             groups = range(half * HALF // GROUP, (half + 1) * HALF // GROUP)
             for c in groups:
-                banks[c] = psum.tile([P, 4, GROUP], F32, tag="bank", name=f"logit{c}")
-            for c, a in [(c, 1) for c in groups] + [(c, a) for c in groups for a in (0, 2)]:
-                plane = (query_planes[TITLE_ROW:P], query_planes[:], body2_plane[:].bitcast(U8))[a]
+                banks[c] = psum.tile([P, 4, GROUP], F32, tag=f"bank{c}", name=f"logit{c}")
+            for c, a in [(c, order[0]) for c in groups] + ([(c, a) for c in groups for a in order[1:]] if half == 0 else [(c, a) for a in order[1:] for c in groups]):
+                plane = query_planes[:] if a == 0 else body_planes[:, a - 1, :].bitcast(U8)
                 inside = slice(c * GROUP % HALF, c * GROUP % HALF + GROUP)
                 for t in range(4):
                     if a == 0:
@@ -172,42 +176,64 @@ def tile_list_sparse_lexical_scores_kernel(
                         lhsT_scale=weight_scales,
                         rhs=query_codes[a, half][:, inside].bitcast(FP8X4),
                         rhs_scale=plane[:, c * GROUP : (c + 1) * GROUP],
-                        start=(a == 1 and t == 0),
-                        stop=(a == 2 and t == 3),
+                        start=(a == order[0] and t == 0),
+                        stop=(a == order[2] and t == 3),
                     )
 
         h_codes = keep.tile([P, S], U32, align_bytes=64)
         h_plane = keep.tile([P, S], U8, align_bytes=64)
         logs = {}
+        h_bf = {}
 
-        def saturate(c):
-            pos = work.tile([P, CHUNK, 4], F32, name="pos")
+        def saturate(c, pos_tag, log_tag):
+            pos = keep.tile([P, CHUNK, 4], F32, name=f"pos{c}", tag=pos_tag, align_bytes=64)
             for e in range(CHUNK // GROUP):
                 nc.scalar.activation(
                     pos[:, e * GROUP : (e + 1) * GROUP, :],
                     banks[c * CHUNK // GROUP + e][:].rearrange("p t n -> p n t"),
                     ACT.Relu,
                 )
-            logs[c] = work.tile([P, CHUNK, 4], F32, name="logs")
+            logs[c] = keep.tile([P, CHUNK, 4], F32, name=f"logs{c}", tag=log_tag, align_bytes=64)
             nc.scalar.activation(logs[c][:], pos[:], ACT.Ln, bias=1.0)
 
+        def apply_gain(c, tag):
+            h_bf[c] = keep.tile([P, CHUNK, 4], BF16, name=f"h_bf{c}", tag=tag, align_bytes=64)
+            nc.vector.tensor_tensor(h_bf[c][:], logs[c][:], gain[:].unsqueeze(1).to_broadcast([P, CHUNK, 4]), ALU.mult)
+
         def quantize_h(c):
-            h_bf = keep.tile([P, CHUNK, 4], BF16, name=f"h_bf{c}", tag="doc_words" if c == 1 else f"h_bf{c}", align_bytes=64)
-            nc.vector.tensor_tensor(h_bf[:], logs[c][:], gain[:].unsqueeze(1).to_broadcast([P, CHUNK, 4]), ALU.mult)
             at = slice(c * CHUNK, (c + 1) * CHUNK)
             nc.vector.quantize_mx(
-                out=h_codes[:, at].bitcast(FP8X4), scales=h_plane[:, at], in_=h_bf[:].rearrange("p n t -> p (n t)")
+                out=h_codes[:, at].bitcast(FP8X4), scales=h_plane[:, at], in_=h_bf[c][:].rearrange("p n t -> p (n t)")
             )
 
-        def scores(c, pair, on_vector):
+        def wide_scores(half, m, on_vector, slot):
+            at = slice(half * HALF, (half + 1) * HALF)
+            bank = psum.tile([P, HALF], F32, tag=f"bank{slot}", name=f"score{half + 8}{m}")
+            nc.tensor.matmul_mx(
+                out=bank[:],
+                lhsT=cand_codes[m // 4][:, m % 4 * P : (m % 4 + 1) * P].bitcast(FP8X4),
+                lhsT_scale=cand_plane[:].bitcast(U8)[:, m * P : (m + 1) * P],
+                rhs=h_codes[:, at].bitcast(FP8X4),
+                rhs_scale=h_plane[:, at],
+                start=True,
+                stop=True,
+            )
+            result = stage.tile([P, HALF], F32, name="result")
+            if on_vector:
+                nc.vector.tensor_scalar(result[:], bank[:], prior_cols[:, m : m + 1], None, ALU.add)
+            else:
+                nc.scalar.activation(result[:], bank[:], ACT.Identity, bias=prior_cols[:, m : m + 1])
+            nc.sync.dma_start(out[m * P : (m + 1) * P, at], result[:])
+
+        def scores(c, pair, on_vector, slot):
             at = slice(c * CHUNK, (c + 1) * CHUNK)
-            bank = psum.tile([P, 2, CHUNK], F32, tag="bank", name=f"score{c}{pair}")
+            bank = psum.tile([P, 2, CHUNK], F32, tag=f"bank{slot}", name=f"score{c}{pair}")
             for e in range(2):
                 rows = slice((2 * pair + e) * P, (2 * pair + e + 1) * P)
                 nc.tensor.matmul_mx(
                     out=bank[:, e, :],
-                    lhsT=cand_codes[:, rows].bitcast(FP8X4),
-                    lhsT_scale=cand_scales[pair // 2][DOC_ROW:P, rows.start % HALF : rows.start % HALF + P],
+                    lhsT=cand_codes[pair // 2][:, rows.start % HALF : rows.start % HALF + P].bitcast(FP8X4),
+                    lhsT_scale=cand_plane[:].bitcast(U8)[:, rows],
                     rhs=h_codes[:, at].bitcast(FP8X4),
                     rhs_scale=h_plane[:, at],
                     start=True,
@@ -224,38 +250,54 @@ def tile_list_sparse_lexical_scores_kernel(
             rows = out[2 * pair * P : 2 * (pair + 1) * P, at]
             nc.sync.dma_start(rows.rearrange("(e p) n -> p e n", e=2), result[:])
 
-        logits(0)
-
-        title_second = keep.tile([P, HALF], U32, align_bytes=64)
-        gather_query_words(0, 1, title_second[:])
-        cand_scales[1] = keep.tile([P, HALF], U8, name="cand_scales1", align_bytes=64, tag="words0")
-        gather_doc_scales(0)
-        body2_second = keep.tile([P, HALF], U32, align_bytes=64, tag="body2_codes")
-        gather_query_words(2, 1, body2_second[:])
-        logits(1)
-
-        nc.vector.transpose(prior_turned[:], prior_rows[:])
-        for q in range(4):
-            quadrant = slice(QUAD * q, QUAD * (q + 1))
-            nc.vector.tensor_copy(prior_cols[quadrant, :], prior_turned[quadrant, q:QUAD:4])
-
-        gather_doc_scales(1)
-        saturate(0)
-        gather_doc_words(0)
+        turn_prior()
+        order_w4_words()
+        nc.vector.tensor_copy(cand_rows[:], doc_rows[:].bitcast(U8).indirect(idx2[:]))
+        gather_query_scales()
+        nc.sync.dma_start(doc_words[:], tab2_words[0].rearrange("p t i -> p (t i)").bitcast(I32))
+        for r in range(4):
+            nc.sync.dma_start(cand_plane[r:P:QUAD, :], cand_rows[8 * r : P : QUAD, :].bitcast(I32))
+        round_w1()
+        w1_codes = keep.tile([P, H], U32, align_bytes=64, tag="w1_codes")
+        nc.vector.quantize_mx(out=w1_codes[:].bitcast(FP8X4), scales=w1_plane[:], in_=w1_bf[:])
+        gather_query_words(0, 0, "codes00")
+        gather_query_words(1, 0, "codes10")
+        order_w4_scales()
+        gather_query_words(2, 0, "codes20", 2)
+        logits(0, (0, 1, 2))
+        gather_query_words(2, 1, "codes21")
+        second = keep.tile([P, 2, HALF], U32, tag="words2", align_bytes=64)
+        for a in (0, 1):
+            query_codes[a, 1] = second[:, a, :]
+            nc.vector.tensor_copy(second[:, a, :], text_words[a][:].bitcast(U32).indirect(idx[:, list_cols(1)]))
+        logits(1, (2, 0, 1))
+        saturate(0, "pos0", "logs0")
+        apply_gain(0, "h_bf0")
+        gather_doc_words(0, "cand_codes0")
         quantize_h(0)
-        gather_doc_words(1)
-        saturate(1)
+        scores(0, 0, False, 0)
+        scores(0, 1, False, 1)
+        saturate(1, "pos1", "logs1x")
+        apply_gain(1, "h_bf1")
+        gather_doc_words(1, "logs1x")
         quantize_h(1)
-        scores(0, 0, False)
-        scores(0, 1, False)
-        saturate(2)
+        saturate(2, "pos1", "logs0")
+        apply_gain(2, "h_bf2")
+        scores(1, 0, True, 2)
         quantize_h(2)
-        saturate(3)
+        scores(1, 1, True, 3)
+        saturate(3, "pos1", "logs1")
+        wide_scores(0, 4, True, 0)
+        apply_gain(3, "h_bf3")
+        wide_scores(0, 5, True, 1)
         quantize_h(3)
-        scores(0, 2, True)
-        scores(0, 3, True)
-        for pair in range(4):
-            scores(1, pair, False)
-        for c in (2, 3):
-            for pair in range(4):
-                scores(c, pair, pair % 2 == 0)
+        wide_scores(0, 6, False, 2)
+        wide_scores(0, 7, False, 3)
+        scores(2, 0, False, 4)
+        scores(2, 1, True, 5)
+        scores(2, 2, False, 6)
+        scores(2, 3, True, 7)
+        scores(3, 0, False, 0)
+        scores(3, 1, True, 1)
+        scores(3, 2, False, 2)
+        scores(3, 3, True, 3)

@@ -196,9 +196,9 @@ def tile_list_sparse_lexical_scores_kernel(
             logs[c] = keep.tile([P, CHUNK, 4], F32, name=f"logs{c}", tag=log_tag, align_bytes=64)
             nc.scalar.activation(logs[c][:], pos[:], ACT.Ln, bias=1.0)
 
-        def apply_gain(c, tag):
+        def apply_gain(c, tag, engine=nc.vector):
             h_bf[c] = keep.tile([P, CHUNK, 4], BF16, name=f"h_bf{c}", tag=tag, align_bytes=64)
-            nc.vector.tensor_tensor(h_bf[c][:], logs[c][:], gain[:].unsqueeze(1).to_broadcast([P, CHUNK, 4]), ALU.mult)
+            engine.tensor_tensor(h_bf[c][:], logs[c][:], gain[:].unsqueeze(1).to_broadcast([P, CHUNK, 4]), ALU.mult)
 
         def quantize_h(c):
             at = slice(c * CHUNK, (c + 1) * CHUNK)
@@ -272,7 +272,7 @@ def tile_list_sparse_lexical_scores_kernel(
             nc.vector.tensor_copy(second[:, a, :], text_words[a][:].bitcast(U32).indirect(idx[:, list_cols(1)]))
         logits(1, (2, 0, 1))
         saturate(0, "pos0", "logs0")
-        apply_gain(0, "h_bf0")
+        apply_gain(0, "h_bf0", nc.gpsimd)
         gather_doc_words(0, "cand_codes0")
         quantize_h(0)
         scores(0, 0, False, 0)

@@ -44,7 +44,7 @@ def tile_list_sparse_lexical_scores_kernel(
         text_planes = keep.tile([P, T // 4], I32, align_bytes=64, tag="text_planes")
         doc_rows = keep.tile([P, T2 // 4], I32, align_bytes=64)
         cand_plane = keep.tile([P, S2 // 4], I32, align_bytes=64)
-        doc_words = keep.tile([P, T2], I32, align_bytes=64)
+        doc_words = keep.tile([P, T2], I32, align_bytes=64, tag="doc_words")
         w4_raw = keep.tile([P, 2, H // 2], I32, align_bytes=64)
         w4_scales_raw = keep.tile([P, 2, H // 4], I32, align_bytes=64)
         gain = keep.tile([P, 4], F32)
@@ -180,7 +180,7 @@ def tile_list_sparse_lexical_scores_kernel(
                         stop=(a == order[2] and t == 3),
                     )
 
-        h_codes = keep.tile([P, S], U32, align_bytes=64)
+        h_codes = keep.tile([P, S], U32, align_bytes=64, tag="doc_words")
         h_plane = keep.tile([P, S], U8, align_bytes=64)
         logs = {}
         h_bf = {}
@@ -274,25 +274,25 @@ def tile_list_sparse_lexical_scores_kernel(
         saturate(0, "pos0", "logs0")
         apply_gain(0, "h_bf0", nc.gpsimd)
         gather_doc_words(0, "cand_codes0")
+        gather_doc_words(1, "cand_codes1")
         quantize_h(0)
+        saturate(1, "pos1", "logs1")
+        apply_gain(1, "h_bf0")
+        quantize_h(1)
         scores(0, 0, False, 0)
         scores(0, 1, False, 1)
-        saturate(1, "pos1", "logs1x")
-        apply_gain(1, "h_bf1")
-        gather_doc_words(1, "logs1x")
-        quantize_h(1)
         saturate(2, "pos1", "logs0")
+        scores(0, 2, True, 2)
+        scores(0, 3, True, 3)
         apply_gain(2, "h_bf2")
-        scores(1, 0, True, 2)
+        scores(1, 0, True, 0)
         quantize_h(2)
-        scores(1, 1, True, 3)
-        saturate(3, "pos1", "logs1")
-        wide_scores(0, 4, True, 0)
+        saturate(3, "h_bf0", "logs1")
+        scores(1, 1, True, 1)
         apply_gain(3, "h_bf3")
-        wide_scores(0, 5, True, 1)
+        scores(1, 2, True, 2)
         quantize_h(3)
-        wide_scores(0, 6, False, 2)
-        wide_scores(0, 7, False, 3)
+        scores(1, 3, False, 3)
         scores(2, 0, False, 4)
         scores(2, 1, True, 5)
         scores(2, 2, False, 6)

@@ -34,7 +34,8 @@ def tile_list_sparse_lexical_scores_kernel(
     nc = tc.nc
     with ExitStack() as ctx:
         keep = ctx.enter_context(tc.tile_pool(name="keep", bufs=1))
-        stage = ctx.enter_context(tc.tile_pool(name="stage", bufs=8))
+        placed = ctx.enter_context(tc.tile_pool(name="placed", bufs=1))
+        stage = ctx.enter_context(tc.tile_pool(name="stage", bufs=16))
         psum = ctx.enter_context(tc.psum_pool(name="psum", bufs=1))
 
         idx = keep.tile([P, S // LIST], U16)
@@ -44,9 +45,8 @@ def tile_list_sparse_lexical_scores_kernel(
         text_planes = keep.tile([P, T // 4], I32, align_bytes=64, tag="text_planes")
         doc_rows = keep.tile([P, T2 // 4], I32, align_bytes=64)
         cand_plane = keep.tile([P, S2 // 4], I32, align_bytes=64)
-        doc_words = keep.tile([P, T2], I32, align_bytes=64, tag="doc_words")
         w4_raw = keep.tile([P, 2, H // 2], I32, align_bytes=64)
-        w4_scales_raw = keep.tile([P, 2, H // 4], I32, align_bytes=64)
+        w4_scales_raw = keep.tile([P, 2, H // 4], I32, align_bytes=64, tag="doc_words")
         gain = keep.tile([P, 4], F32)
         prior_rows = keep.tile([P, QUAD], F32, align_bytes=64)
         prior_turned = keep.tile([P, QUAD], F32, align_bytes=64)
@@ -77,11 +77,11 @@ def tile_list_sparse_lexical_scores_kernel(
         load_title_scales(nc.sync, 0)
         load_title_scales(nc.sync, 1)
         load_text_words(0)
-        load_text_words(1)
         nc.sync.dma_start(w4_scales_raw[0:P:QUAD], w4_scales[:, 0:16:4, :].rearrange("a q n -> q a n").bitcast(I32))
         nc.sync.dma_start(w4_scales_raw[1:P:QUAD], w4_scales[:, 1:16:4, :].rearrange("a q n -> q a n").bitcast(I32))
         nc.sync.dma_start(w4_scales_raw[2:P:QUAD], w4_scales[:, 2:16:4, :].rearrange("a q n -> q a n").bitcast(I32))
         nc.sync.dma_start(w4_scales_raw[3:P:QUAD], w4_scales[:, 3:16:4, :].rearrange("a q n -> q a n").bitcast(I32))
+        load_text_words(1)
         load_text_words(2)
         nc.scalar.dma_start(w4_raw[:], w4_words.rearrange("a p n -> p a n").bitcast(I32))
         nc.scalar.dma_start(
@@ -111,7 +111,10 @@ def tile_list_sparse_lexical_scores_kernel(
                 nc.vector.tensor_copy(codes[:, first : first + width], window.indirect(idx[:, entries]))
 
         def gather_doc_words(half, tag):
-            cand_codes[half] = keep.tile([P, HALF], U32, name=f"cand_codes{half}", tag=tag, align_bytes=64)
+            if half == 1:
+                cand_codes[half] = placed.tile([P, HALF], U32, name="cand_codes1", align_bytes=64, offset=4096)
+            else:
+                cand_codes[half] = keep.tile([P, HALF], U32, name=f"cand_codes{half}", tag=tag, align_bytes=64)
             window = doc_words[:].bitcast(U32)
             nc.vector.tensor_copy(cand_codes[half][:], window.indirect(idx2[:, list_cols(half)]))
 
@@ -156,11 +159,11 @@ def tile_list_sparse_lexical_scores_kernel(
 
         banks = {}
 
-        def logits(half, order):
-            groups = range(half * HALF // GROUP, (half + 1) * HALF // GROUP)
-            for c in groups:
-                banks[c] = psum.tile([P, 4, GROUP], F32, tag=f"bank{c}", name=f"logit{c}")
-            for c, a in [(c, order[0]) for c in groups] + ([(c, a) for c in groups for a in order[1:]] if half == 0 else [(c, a) for a in order[1:] for c in groups]):
+        def logits(steps, first_pass, last_pass):
+            for c, a in steps:
+                half = c * GROUP // HALF
+                if a == first_pass:
+                    banks[c] = psum.tile([P, 4, GROUP], F32, tag=f"bank{c}", name=f"logit{c}")
                 plane = query_planes[:] if a == 0 else body_planes[:, a - 1, :].bitcast(U8)
                 inside = slice(c * GROUP % HALF, c * GROUP % HALF + GROUP)
                 for t in range(4):
@@ -176,29 +179,35 @@ def tile_list_sparse_lexical_scores_kernel(
                         lhsT_scale=weight_scales,
                         rhs=query_codes[a, half][:, inside].bitcast(FP8X4),
                         rhs_scale=plane[:, c * GROUP : (c + 1) * GROUP],
-                        start=(a == order[0] and t == 0),
-                        stop=(a == order[2] and t == 3),
+                        start=(a == first_pass and t == 0),
+                        stop=(a == last_pass and t == 3),
                     )
 
-        h_codes = keep.tile([P, S], U32, align_bytes=64, tag="doc_words")
         h_plane = keep.tile([P, S], U8, align_bytes=64)
         logs = {}
         h_bf = {}
 
         def saturate(c, pos_tag, log_tag):
-            pos = keep.tile([P, CHUNK, 4], F32, name=f"pos{c}", tag=pos_tag, align_bytes=64)
-            for e in range(CHUNK // GROUP):
-                nc.scalar.activation(
-                    pos[:, e * GROUP : (e + 1) * GROUP, :],
-                    banks[c * CHUNK // GROUP + e][:].rearrange("p t n -> p n t"),
-                    ACT.Relu,
-                )
+            if c == 1:
+                pos = placed.tile([P, CHUNK, 4], F32, name="pos1", align_bytes=64, offset=2048)
+            else:
+                pos = keep.tile([P, CHUNK, 4], F32, name=f"pos{c}", tag=pos_tag, align_bytes=64)
             logs[c] = keep.tile([P, CHUNK, 4], F32, name=f"logs{c}", tag=log_tag, align_bytes=64)
-            nc.scalar.activation(logs[c][:], pos[:], ACT.Ln, bias=1.0)
+            for e in range(CHUNK // GROUP):
+                group = slice(e * GROUP, (e + 1) * GROUP)
+                bank = banks[c * CHUNK // GROUP + e]
+                nc.scalar.activation(pos[:, group, :], bank[:].rearrange("p t n -> p n t"), ACT.Relu)
+            for first in range(0, CHUNK, GROUP):
+                part = slice(first, first + GROUP)
+                nc.scalar.activation(logs[c][:, part, :], pos[:, part, :], ACT.Ln, bias=1.0)
 
         def apply_gain(c, tag, engine=nc.vector):
             h_bf[c] = keep.tile([P, CHUNK, 4], BF16, name=f"h_bf{c}", tag=tag, align_bytes=64)
-            engine.tensor_tensor(h_bf[c][:], logs[c][:], gain[:].unsqueeze(1).to_broadcast([P, CHUNK, 4]), ALU.mult)
+            width = GROUP if c in (0,) else CHUNK
+            for first in range(0, CHUNK, width):
+                part = slice(first, first + width)
+                gains = gain[:].unsqueeze(1).to_broadcast([P, width, 4])
+                engine.tensor_tensor(h_bf[c][:, part, :], logs[c][:, part, :], gains, ALU.mult)
 
         def quantize_h(c):
             at = slice(c * CHUNK, (c + 1) * CHUNK)
@@ -254,50 +263,53 @@ def tile_list_sparse_lexical_scores_kernel(
         order_w4_words()
         nc.vector.tensor_copy(cand_rows[:], doc_rows[:].bitcast(U8).indirect(idx2[:]))
         gather_query_scales()
-        nc.sync.dma_start(doc_words[:], tab2_words[0].rearrange("p t i -> p (t i)").bitcast(I32))
         for r in range(4):
             nc.sync.dma_start(cand_plane[r:P:QUAD, :], cand_rows[8 * r : P : QUAD, :].bitcast(I32))
         round_w1()
         w1_codes = keep.tile([P, H], U32, align_bytes=64, tag="w1_codes")
         nc.vector.quantize_mx(out=w1_codes[:].bitcast(FP8X4), scales=w1_plane[:], in_=w1_bf[:])
         gather_query_words(0, 0, "codes00")
-        gather_query_words(1, 0, "codes10")
         order_w4_scales()
+        doc_words = keep.tile([P, T2], I32, align_bytes=64, tag="doc_words")
+        nc.scalar.dma_start(doc_words[:], tab2_words[0].rearrange("p t i -> p (t i)").bitcast(I32))
+        gather_query_words(1, 0, "codes10")
         gather_query_words(2, 0, "codes20", 2)
-        logits(0, (0, 1, 2))
+        logits([(c, 0) for c in range(4)] + [(c, a) for c in range(4) for a in (1, 2)], 0, 2)
         gather_query_words(2, 1, "codes21")
         second = keep.tile([P, 2, HALF], U32, tag="words2", align_bytes=64)
         for a in (0, 1):
             query_codes[a, 1] = second[:, a, :]
             nc.vector.tensor_copy(second[:, a, :], text_words[a][:].bitcast(U32).indirect(idx[:, list_cols(1)]))
-        logits(1, (2, 0, 1))
+        logits([(c, a) for a in (2, 0) for c in range(4, 8)] + [(4, 1), (5, 1)], 2, 1)
         saturate(0, "pos0", "logs0")
         apply_gain(0, "h_bf0", nc.gpsimd)
-        gather_doc_words(0, "cand_codes0")
-        gather_doc_words(1, "cand_codes1")
-        quantize_h(0)
         saturate(1, "pos1", "logs1")
-        apply_gain(1, "h_bf0")
-        quantize_h(1)
-        scores(0, 0, False, 0)
-        scores(0, 1, False, 1)
-        saturate(2, "pos1", "logs0")
+        gather_doc_words(0, "cand_codes0")
+        h_codes = keep.tile([P, S], U32, align_bytes=64)
+        quantize_h(0)
+        gather_doc_words(1, "cand_codes1")
+        apply_gain(1, "h_bf0", nc.gpsimd)
+        saturate(2, "pos2", "logs2")
+        scores(0, 0, True, 0)
+        scores(0, 1, True, 1)
         scores(0, 2, True, 2)
+        logits([(6, 1), (7, 1)], 2, 1)
+        quantize_h(1)
         scores(0, 3, True, 3)
-        apply_gain(2, "h_bf2")
-        scores(1, 0, True, 0)
+        saturate(3, "pos3", "logs3")
+        apply_gain(2, "h_bf0")
         quantize_h(2)
-        saturate(3, "h_bf0", "logs1")
-        scores(1, 1, True, 1)
         apply_gain(3, "h_bf3")
-        scores(1, 2, True, 2)
         quantize_h(3)
-        scores(1, 3, False, 3)
-        scores(2, 0, False, 4)
-        scores(2, 1, True, 5)
-        scores(2, 2, False, 6)
-        scores(2, 3, True, 7)
-        scores(3, 0, False, 0)
-        scores(3, 1, True, 1)
-        scores(3, 2, False, 2)
-        scores(3, 3, True, 3)
+        scores(1, 0, False, 4)
+        scores(1, 1, True, 5)
+        scores(1, 2, False, 6)
+        scores(1, 3, False, 7)
+        scores(2, 0, False, 0)
+        scores(2, 1, True, 1)
+        scores(2, 2, False, 2)
+        scores(2, 3, True, 3)
+        scores(3, 0, False, 4)
+        scores(3, 1, True, 5)
+        scores(3, 2, False, 6)
+        scores(3, 3, True, 7)

@@ -15,16 +15,19 @@ ALU = mybir.AluOpType
 
 P = 128
 QUAD = 32
+PACK = 4
+BLOCKS = 16
+BANKS = 8
 K, H = 1536, 512
 T, S = 2048, 1024
 T2, S2 = 4096, 1024
+TITLE, BODY1, BODY2 = 0, 1, 2
 HALF = 512
 CHUNK = 256
 GROUP = 128
 LIST = 16
-BODY2_ROW, TITLE_ROW = 16, 8
-DOC_ROW = 12
-PLANE_ROWS = 3 * QUAD + 4
+PLANE_ROWS = 3 * QUAD + PACK
+SPREAD = P // BLOCKS
 FLOPS = 2 * K * H * S + 2 * H * S2 * S
 
 
@@ -34,20 +37,19 @@ def tile_list_sparse_lexical_scores_kernel(
     nc = tc.nc
     with ExitStack() as ctx:
         keep = ctx.enter_context(tc.tile_pool(name="keep", bufs=1))
-        placed = ctx.enter_context(tc.tile_pool(name="placed", bufs=1))
-        stage = ctx.enter_context(tc.tile_pool(name="stage", bufs=16))
+        stage = ctx.enter_context(tc.tile_pool(name="stage", bufs=S * S2 // (P * HALF)))
         psum = ctx.enter_context(tc.psum_pool(name="psum", bufs=1))
 
         idx = keep.tile([P, S // LIST], U16)
         idx2 = keep.tile([P, S2 // LIST], U16)
         text_words = [keep.tile([P, T], I32, name=f"words{a}", tag=f"words{a}", align_bytes=64) for a in range(3)]
-        w1_raw = keep.tile([P, 4, H], F32, align_bytes=64, tag="w1_raw")
-        text_planes = keep.tile([P, T // 4], I32, align_bytes=64, tag="text_planes")
+        w1_raw = keep.tile([P, PACK, H], F32, align_bytes=64)
+        text_planes = keep.tile([P, T // 4], I32, align_bytes=64)
         doc_rows = keep.tile([P, T2 // 4], I32, align_bytes=64)
         cand_plane = keep.tile([P, S2 // 4], I32, align_bytes=64)
         w4_raw = keep.tile([P, 2, H // 2], I32, align_bytes=64)
         w4_scales_raw = keep.tile([P, 2, H // 4], I32, align_bytes=64, tag="doc_words")
-        gain = keep.tile([P, 4], F32)
+        gain = keep.tile([P, PACK], F32)
         prior_rows = keep.tile([P, QUAD], F32, align_bytes=64)
         prior_turned = keep.tile([P, QUAD], F32, align_bytes=64)
         prior_cols = keep.tile([P, S2 // P], F32)
@@ -64,252 +66,213 @@ def tile_list_sparse_lexical_scores_kernel(
         def load_text_words(a):
             nc.sync.dma_start(text_words[a][:], tab_words[a].rearrange("p t i -> p (t i)").bitcast(I32))
 
-        def load_body_scales(queue, q):
-            rows = tab_scales[1:3, q:16:4, :].rearrange("a q n -> q a n")
-            queue.dma_start(text_planes[q:P:BODY2_ROW, :], rows.bitcast(I32))
-
-        def load_title_scales(queue, r):
-            queue.dma_start(text_planes[QUAD * r : QUAD * r + 12, :], tab_scales[:, 4 * r : 4 * r + 4, :].bitcast(I32))
+        def load_text_scales(queue, q):
+            rows = tab_scales[:, PACK * q : PACK * (q + 1), :].bitcast(I32)
+            queue.dma_start(text_planes[QUAD * q : QUAD * q + 3 * PACK, :], rows)
 
         nc.sync.dma_start(idx2[:], offs2)
         nc.sync.dma_start(idx[:], offs)
-        nc.sync.dma_start(w1_raw[:], w1.rearrange("(p j) c -> p j c", j=4))
-        load_title_scales(nc.sync, 0)
-        load_title_scales(nc.sync, 1)
-        load_text_words(0)
-        nc.sync.dma_start(w4_scales_raw[0:P:QUAD], w4_scales[:, 0:16:4, :].rearrange("a q n -> q a n").bitcast(I32))
-        nc.sync.dma_start(w4_scales_raw[1:P:QUAD], w4_scales[:, 1:16:4, :].rearrange("a q n -> q a n").bitcast(I32))
-        nc.sync.dma_start(w4_scales_raw[2:P:QUAD], w4_scales[:, 2:16:4, :].rearrange("a q n -> q a n").bitcast(I32))
-        nc.sync.dma_start(w4_scales_raw[3:P:QUAD], w4_scales[:, 3:16:4, :].rearrange("a q n -> q a n").bitcast(I32))
-        load_text_words(1)
-        load_text_words(2)
+        nc.sync.dma_start(w1_raw[:], w1.rearrange("(p j) c -> p j c", j=PACK))
+        load_text_scales(nc.sync, 0)
+        load_text_scales(nc.sync, 1)
+        load_text_words(TITLE)
+        for r in range(PACK):
+            rows = w4_scales[:, r:BLOCKS:PACK, :].rearrange("a q n -> q a n").bitcast(I32)
+            nc.sync.dma_start(w4_scales_raw[r:P:QUAD], rows)
+        load_text_words(BODY1)
+        load_text_words(BODY2)
         nc.scalar.dma_start(w4_raw[:], w4_words.rearrange("a p n -> p a n").bitcast(I32))
         nc.scalar.dma_start(
-            prior_rows[:], prior.rearrange("(r b) -> r b", b=QUAD).unsqueeze(0).to_broadcast([4, QUAD, QUAD])
+            prior_rows[:], prior.rearrange("(r b) -> r b", b=QUAD).unsqueeze(0).to_broadcast([P // QUAD, QUAD, QUAD])
         )
-        nc.scalar.dma_start(doc_rows[0:P:8, :], tab2_scales[0].bitcast(I32))
-        load_title_scales(nc.scalar, 2)
-        load_title_scales(nc.scalar, 3)
-        nc.scalar.dma_start(gain[:], g.rearrange("(p t) -> p t", t=4))
+        nc.scalar.dma_start(doc_rows[0:P:SPREAD, :], tab2_scales[0].bitcast(I32))
+        load_text_scales(nc.scalar, 2)
+        load_text_scales(nc.scalar, 3)
+        nc.scalar.dma_start(gain[:], g.rearrange("(p t) -> p t", t=PACK))
         nc.scalar.activation(warm[:, 1:2], warm[:, 0:1], ACT.Ln, bias=1.0)
 
-        query_planes = keep.tile([P, S], U8, align_bytes=64)
-        cand_codes = {}
-        query_codes = {}
-        cand_rows = keep.tile([P, S2], U8, align_bytes=64)
+        def entries(first, count):
+            return slice(first // LIST, (first + count) // LIST)
 
-        def list_cols(half):
-            return slice(half * HALF // LIST, (half + 1) * HALF // LIST)
+        def gather_words(codes, table, offsets):
+            nc.vector.tensor_copy(codes, table[:].bitcast(U32).indirect(offsets))
 
-        def gather_query_words(a, half, tag, pieces=1):
-            codes = keep.tile([P, HALF], U32, name=f"codes{a}{half}", tag=tag, align_bytes=64)
-            query_codes[a, half] = codes
-            width = HALF // pieces
-            for first in range(0, HALF, width):
-                entries = slice((half * HALF + first) // LIST, (half * HALF + first + width) // LIST)
-                window = text_words[a][:].bitcast(U32)
-                nc.vector.tensor_copy(codes[:, first : first + width], window.indirect(idx[:, entries]))
-
-        def gather_doc_words(half, tag):
-            if half == 1:
-                cand_codes[half] = placed.tile([P, HALF], U32, name="cand_codes1", align_bytes=64, offset=4096)
-            else:
-                cand_codes[half] = keep.tile([P, HALF], U32, name=f"cand_codes{half}", tag=tag, align_bytes=64)
-            window = doc_words[:].bitcast(U32)
-            nc.vector.tensor_copy(cand_codes[half][:], window.indirect(idx2[:, list_cols(half)]))
-
-        def gather_query_scales():
-            nc.vector.tensor_copy(query_planes[:], text_planes[:].bitcast(U8).indirect(idx[:]))
-            for a in (1, 2):
-                nc.sync.dma_start(
-                    body_planes[0:PLANE_ROWS, a - 1, :], query_planes[4 * a : 4 * a + PLANE_ROWS, :].bitcast(I32)
-                )
+        nc.vector.transpose(prior_turned[:], prior_rows[:])
+        for q in range(P // QUAD):
+            quadrant = slice(QUAD * q, QUAD * (q + 1))
+            nc.vector.tensor_copy(prior_cols[quadrant, :], prior_turned[quadrant, q : QUAD : P // QUAD])
 
         w4_codes = keep.tile([P, 2, 2 * H], U8, align_bytes=64)
-        w4_planes = keep.tile([P, 2, H], U8, align_bytes=64)
+        nc.vector.tensor_copy(
+            w4_codes[:].bitcast(U16).rearrange("p a (t m) -> p a t m", t=PACK),
+            w4_raw[:].bitcast(U16).rearrange("p a (m t) -> p a t m", t=PACK),
+        )
 
-        def order_w4_words():
-            nc.vector.tensor_copy(
-                w4_codes[:].bitcast(U16).rearrange("p a (t m) -> p a t m", t=4),
-                w4_raw[:].bitcast(U16).rearrange("p a (m t) -> p a t m", t=4),
-            )
+        cand_rows = keep.tile([P, S2], U8, align_bytes=64)
+        nc.vector.tensor_copy(cand_rows[:], doc_rows[:].bitcast(U8).indirect(idx2[:]))
 
-        def order_w4_scales():
-            nc.vector.tensor_copy(
-                w4_planes[:].rearrange("p a (t m) -> p a t m", t=4),
-                w4_scales_raw[:].bitcast(U8).rearrange("p a (m t) -> p a t m", t=4),
-            )
+        query_planes = keep.tile([P, S], U8, align_bytes=64)
+        nc.vector.tensor_copy(query_planes[:], text_planes[:].bitcast(U8).indirect(idx[:]))
+        for a in (BODY1, BODY2):
+            rows = query_planes[PACK * a : PACK * a + PLANE_ROWS, :].bitcast(I32)
+            nc.sync.dma_start(body_planes[0:PLANE_ROWS, a - BODY1, :], rows)
+        for r in range(PACK):
+            nc.sync.dma_start(cand_plane[r:P:QUAD, :], cand_rows[SPREAD * r : P : QUAD, :].bitcast(I32))
 
-        w1_bf = keep.tile([P, 4 * H], BF16, align_bytes=64, tag="w1_bf")
+        w1_bf = keep.tile([P, PACK * H], BF16, align_bytes=64)
+        w1_codes = keep.tile([P, H], U32, align_bytes=64)
         w1_plane = keep.tile([P, H], U8, align_bytes=64)
+        for tiles in (slice(0, 2), slice(2, 4)):
+            nc.scalar.activation(
+                w1_bf[:].rearrange("p (t m j) -> p m j t", t=PACK, j=PACK)[:, :, :, tiles],
+                w1_raw[:].rearrange("p j (m t) -> p m j t", t=PACK)[:, :, :, tiles],
+                ACT.Identity,
+            )
+        nc.vector.quantize_mx(out=w1_codes[:].bitcast(FP8X4), scales=w1_plane[:], in_=w1_bf[:])
 
-        def round_w1():
-            for u in range(2):
-                nc.scalar.activation(
-                    w1_bf[:].rearrange("p (t m j) -> p m j t", t=4, j=4)[:, :, :, 2 * u : 2 * u + 2],
-                    w1_raw[:].rearrange("p j (m t) -> p m j t", t=4)[:, :, :, 2 * u : 2 * u + 2],
-                    ACT.Identity,
-                )
+        query_codes = {}
 
-        def turn_prior():
-            nc.vector.transpose(prior_turned[:], prior_rows[:])
-            for q in range(4):
-                quadrant = slice(QUAD * q, QUAD * (q + 1))
-                nc.vector.tensor_copy(prior_cols[quadrant, :], prior_turned[quadrant, q:QUAD:4])
+        def gather_queries(a, half, width):
+            codes = keep.tile([P, HALF], U32, name=f"codes{a}{half}", align_bytes=64)
+            query_codes[a, half] = codes
+            for first in range(0, HALF, width):
+                gather_words(codes[:, first : first + width], text_words[a], idx[:, entries(half * HALF + first, width)])
 
-        banks = {}
+        gather_queries(TITLE, 0, HALF)
+        w4_planes = keep.tile([P, 2, H], U8, align_bytes=64)
+        nc.vector.tensor_copy(
+            w4_planes[:].rearrange("p a (t m) -> p a t m", t=PACK),
+            w4_scales_raw[:].bitcast(U8).rearrange("p a (m t) -> p a t m", t=PACK),
+        )
+        doc_words = keep.tile([P, T2], I32, align_bytes=64, tag="doc_words")
+        nc.scalar.dma_start(doc_words[:], tab2_words[0].rearrange("p t i -> p (t i)").bitcast(I32))
+        gather_queries(BODY1, 0, HALF)
+        gather_queries(BODY2, 0, CHUNK)
+
+        logit_banks = {}
 
         def logits(steps, first_pass, last_pass):
             for c, a in steps:
-                half = c * GROUP // HALF
                 if a == first_pass:
-                    banks[c] = psum.tile([P, 4, GROUP], F32, tag=f"bank{c}", name=f"logit{c}")
-                plane = query_planes[:] if a == 0 else body_planes[:, a - 1, :].bitcast(U8)
-                inside = slice(c * GROUP % HALF, c * GROUP % HALF + GROUP)
-                for t in range(4):
-                    if a == 0:
+                    logit_banks[c] = psum.tile([P, PACK, GROUP], F32, tag=f"bank{c}", name=f"logit{c}")
+                plane = query_planes[:] if a == TITLE else body_planes[:, a - BODY1, :].bitcast(U8)
+                half, inside = divmod(c * GROUP, HALF)
+                for t in range(PACK):
+                    if a == TITLE:
                         weights = w1_codes[:, P * t : P * (t + 1)].bitcast(FP8X4)
                         weight_scales = w1_plane[:, P * t : P * (t + 1)]
                     else:
-                        weights = w4_codes[:, a - 1, 2 * P * t : 2 * P * (t + 1)].bitcast(FP4X4)
-                        weight_scales = w4_planes[:, a - 1, P * t : P * (t + 1)]
+                        weights = w4_codes[:, a - BODY1, 2 * P * t : 2 * P * (t + 1)].bitcast(FP4X4)
+                        weight_scales = w4_planes[:, a - BODY1, P * t : P * (t + 1)]
                     nc.tensor.matmul_mx(
-                        out=banks[c][:, t, :],
+                        out=logit_banks[c][:, t, :],
                         lhsT=weights,
                         lhsT_scale=weight_scales,
-                        rhs=query_codes[a, half][:, inside].bitcast(FP8X4),
+                        rhs=query_codes[a, half][:, inside : inside + GROUP].bitcast(FP8X4),
                         rhs_scale=plane[:, c * GROUP : (c + 1) * GROUP],
                         start=(a == first_pass and t == 0),
-                        stop=(a == last_pass and t == 3),
+                        stop=(a == last_pass and t == PACK - 1),
                     )
 
+        groups = range(HALF // GROUP)
+        logits([(c, TITLE) for c in groups] + [(c, a) for c in groups for a in (BODY1, BODY2)], TITLE, BODY2)
+
+        gather_queries(BODY2, 1, HALF)
+        late_codes = keep.tile([P, 2, HALF], U32, tag=f"words{BODY2}", align_bytes=64)
+        for a in (TITLE, BODY1):
+            query_codes[a, 1] = late_codes[:, a, :]
+            gather_words(late_codes[:, a, :], text_words[a], idx[:, entries(HALF, HALF)])
+        groups = range(HALF // GROUP, S // GROUP)
+        closing = [(c, BODY1) for c in groups]
+        logits([(c, a) for a in (BODY2, TITLE) for c in groups] + closing[:2], BODY2, BODY1)
+
+        h_codes = keep.tile([P, S], U32, align_bytes=64)
         h_plane = keep.tile([P, S], U8, align_bytes=64)
         logs = {}
-        h_bf = {}
+        cand_codes = {}
 
-        def saturate(c, pos_tag, log_tag):
-            if c == 1:
-                pos = placed.tile([P, CHUNK, 4], F32, name="pos1", align_bytes=64, offset=2048)
-            else:
-                pos = keep.tile([P, CHUNK, 4], F32, name=f"pos{c}", tag=pos_tag, align_bytes=64)
-            logs[c] = keep.tile([P, CHUNK, 4], F32, name=f"logs{c}", tag=log_tag, align_bytes=64)
-            for e in range(CHUNK // GROUP):
-                group = slice(e * GROUP, (e + 1) * GROUP)
-                bank = banks[c * CHUNK // GROUP + e]
-                nc.scalar.activation(pos[:, group, :], bank[:].rearrange("p t n -> p n t"), ACT.Relu)
+        def saturate(c):
+            positive = keep.tile([P, CHUNK, PACK], F32, name=f"positive{c}", tag=f"positive{c}", align_bytes=64)
+            logs[c] = keep.tile([P, CHUNK, PACK], F32, name=f"logs{c}", align_bytes=64)
             for first in range(0, CHUNK, GROUP):
-                part = slice(first, first + GROUP)
-                nc.scalar.activation(logs[c][:, part, :], pos[:, part, :], ACT.Ln, bias=1.0)
+                bank = logit_banks[(c * CHUNK + first) // GROUP]
+                nc.scalar.activation(
+                    positive[:, first : first + GROUP, :], bank[:].rearrange("p t n -> p n t"), ACT.Relu
+                )
+            for first in range(0, CHUNK, GROUP):
+                group = slice(first, first + GROUP)
+                nc.scalar.activation(logs[c][:, group, :], positive[:, group, :], ACT.Ln, bias=1.0)
 
-        def apply_gain(c, tag, engine=nc.vector):
-            h_bf[c] = keep.tile([P, CHUNK, 4], BF16, name=f"h_bf{c}", tag=tag, align_bytes=64)
-            width = GROUP if c in (0,) else CHUNK
+        def apply_gain(engine, c, rounded, width):
+            gains = gain[:].unsqueeze(1).to_broadcast([P, width, PACK])
             for first in range(0, CHUNK, width):
                 part = slice(first, first + width)
-                gains = gain[:].unsqueeze(1).to_broadcast([P, width, 4])
-                engine.tensor_tensor(h_bf[c][:, part, :], logs[c][:, part, :], gains, ALU.mult)
+                engine.tensor_tensor(rounded[:, part, :], logs[c][:, part, :], gains, ALU.mult)
 
-        def quantize_h(c):
-            at = slice(c * CHUNK, (c + 1) * CHUNK)
+        def rounded_tile(queries):
+            return keep.tile([P, queries, PACK], BF16, name="rounded", tag="rounded", align_bytes=64)
+
+        def quantize_h(first, width, rounded):
+            at = slice(first, first + width)
             nc.vector.quantize_mx(
-                out=h_codes[:, at].bitcast(FP8X4), scales=h_plane[:, at], in_=h_bf[c][:].rearrange("p n t -> p (n t)")
+                out=h_codes[:, at].bitcast(FP8X4), scales=h_plane[:, at], in_=rounded[:].rearrange("p n t -> p (n t)")
             )
 
-        def wide_scores(half, m, on_vector, slot):
-            at = slice(half * HALF, (half + 1) * HALF)
-            bank = psum.tile([P, HALF], F32, tag=f"bank{slot}", name=f"score{half + 8}{m}")
-            nc.tensor.matmul_mx(
-                out=bank[:],
-                lhsT=cand_codes[m // 4][:, m % 4 * P : (m % 4 + 1) * P].bitcast(FP8X4),
-                lhsT_scale=cand_plane[:].bitcast(U8)[:, m * P : (m + 1) * P],
-                rhs=h_codes[:, at].bitcast(FP8X4),
-                rhs_scale=h_plane[:, at],
-                start=True,
-                stop=True,
-            )
-            result = stage.tile([P, HALF], F32, name="result")
-            if on_vector:
-                nc.vector.tensor_scalar(result[:], bank[:], prior_cols[:, m : m + 1], None, ALU.add)
-            else:
-                nc.scalar.activation(result[:], bank[:], ACT.Identity, bias=prior_cols[:, m : m + 1])
-            nc.sync.dma_start(out[m * P : (m + 1) * P, at], result[:])
+        def gather_candidates(half, tag):
+            cand_codes[half] = keep.tile([P, HALF], U32, name=f"cand_codes{half}", tag=tag, align_bytes=64)
+            gather_words(cand_codes[half][:], doc_words, idx2[:, entries(half * HALF, HALF)])
 
-        def scores(c, pair, on_vector, slot):
-            at = slice(c * CHUNK, (c + 1) * CHUNK)
-            bank = psum.tile([P, 2, CHUNK], F32, tag=f"bank{slot}", name=f"score{c}{pair}")
-            for e in range(2):
-                rows = slice((2 * pair + e) * P, (2 * pair + e + 1) * P)
+        filled = []
+
+        def scores(first, width, m, on_vector):
+            at = slice(first, first + width)
+            tiles = HALF // width
+            bank = psum.tile([P, tiles, width], F32, tag=f"bank{len(filled) % BANKS}", name=f"score{len(filled)}")
+            filled.append(bank)
+            for e in range(tiles):
+                half, inside = divmod((m + e) * P, HALF)
                 nc.tensor.matmul_mx(
                     out=bank[:, e, :],
-                    lhsT=cand_codes[pair // 2][:, rows.start % HALF : rows.start % HALF + P].bitcast(FP8X4),
-                    lhsT_scale=cand_plane[:].bitcast(U8)[:, rows],
+                    lhsT=cand_codes[half][:, inside : inside + P].bitcast(FP8X4),
+                    lhsT_scale=cand_plane[:].bitcast(U8)[:, (m + e) * P : (m + e + 1) * P],
                     rhs=h_codes[:, at].bitcast(FP8X4),
                     rhs_scale=h_plane[:, at],
                     start=True,
                     stop=True,
                 )
-            result = stage.tile([P, 2, CHUNK], F32, name="result")
+            result = stage.tile([P, tiles, width], F32, name="result")
             if on_vector:
-                priors = prior_cols[:, 2 * pair : 2 * pair + 2].unsqueeze(2).to_broadcast([P, 2, CHUNK])
+                priors = prior_cols[:, m : m + tiles].unsqueeze(2).to_broadcast([P, tiles, width])
                 nc.vector.tensor_tensor(result[:], bank[:], priors, ALU.add)
             else:
-                for e in range(2):
-                    m = 2 * pair + e
-                    nc.scalar.activation(result[:, e, :], bank[:, e, :], ACT.Identity, bias=prior_cols[:, m : m + 1])
-            rows = out[2 * pair * P : 2 * (pair + 1) * P, at]
-            nc.sync.dma_start(rows.rearrange("(e p) n -> p e n", e=2), result[:])
+                for e in range(tiles):
+                    bias = prior_cols[:, m + e : m + e + 1]
+                    nc.scalar.activation(result[:, e, :], bank[:, e, :], ACT.Identity, bias=bias)
+            rows = out[m * P : (m + tiles) * P, at]
+            nc.sync.dma_start(rows.rearrange("(e p) n -> p e n", e=tiles), result[:])
 
-        turn_prior()
-        order_w4_words()
-        nc.vector.tensor_copy(cand_rows[:], doc_rows[:].bitcast(U8).indirect(idx2[:]))
-        gather_query_scales()
-        for r in range(4):
-            nc.sync.dma_start(cand_plane[r:P:QUAD, :], cand_rows[8 * r : P : QUAD, :].bitcast(I32))
-        round_w1()
-        w1_codes = keep.tile([P, H], U32, align_bytes=64, tag="w1_codes")
-        nc.vector.quantize_mx(out=w1_codes[:].bitcast(FP8X4), scales=w1_plane[:], in_=w1_bf[:])
-        gather_query_words(0, 0, "codes00")
-        order_w4_scales()
-        doc_words = keep.tile([P, T2], I32, align_bytes=64, tag="doc_words")
-        nc.scalar.dma_start(doc_words[:], tab2_words[0].rearrange("p t i -> p (t i)").bitcast(I32))
-        gather_query_words(1, 0, "codes10")
-        gather_query_words(2, 0, "codes20", 2)
-        logits([(c, 0) for c in range(4)] + [(c, a) for c in range(4) for a in (1, 2)], 0, 2)
-        gather_query_words(2, 1, "codes21")
-        second = keep.tile([P, 2, HALF], U32, tag="words2", align_bytes=64)
-        for a in (0, 1):
-            query_codes[a, 1] = second[:, a, :]
-            nc.vector.tensor_copy(second[:, a, :], text_words[a][:].bitcast(U32).indirect(idx[:, list_cols(1)]))
-        logits([(c, a) for a in (2, 0) for c in range(4, 8)] + [(4, 1), (5, 1)], 2, 1)
-        saturate(0, "pos0", "logs0")
-        apply_gain(0, "h_bf0", nc.gpsimd)
-        saturate(1, "pos1", "logs1")
-        gather_doc_words(0, "cand_codes0")
-        h_codes = keep.tile([P, S], U32, align_bytes=64)
-        quantize_h(0)
-        gather_doc_words(1, "cand_codes1")
-        apply_gain(1, "h_bf0", nc.gpsimd)
-        saturate(2, "pos2", "logs2")
-        scores(0, 0, True, 0)
-        scores(0, 1, True, 1)
-        scores(0, 2, True, 2)
-        logits([(6, 1), (7, 1)], 2, 1)
-        quantize_h(1)
-        scores(0, 3, True, 3)
-        saturate(3, "pos3", "logs3")
-        apply_gain(2, "h_bf0")
-        quantize_h(2)
-        apply_gain(3, "h_bf3")
-        quantize_h(3)
-        scores(1, 0, False, 4)
-        scores(1, 1, True, 5)
-        scores(1, 2, False, 6)
-        scores(1, 3, False, 7)
-        scores(2, 0, False, 0)
-        scores(2, 1, True, 1)
-        scores(2, 2, False, 2)
-        scores(2, 3, True, 3)
-        scores(3, 0, False, 4)
-        scores(3, 1, True, 5)
-        scores(3, 2, False, 6)
-        scores(3, 3, True, 7)
+        saturate(0)
+        rounded = rounded_tile(CHUNK)
+        apply_gain(nc.gpsimd, 0, rounded, GROUP)
+        saturate(1)
+        gather_candidates(0, "cand_codes0")
+        quantize_h(0, CHUNK, rounded)
+        gather_candidates(1, "positive1")
+        rounded = rounded_tile(CHUNK)
+        apply_gain(nc.gpsimd, 1, rounded, CHUNK)
+        saturate(2)
+        pairs = range(0, S2 // P, HALF // CHUNK)
+        for m in pairs[:-1]:
+            scores(0, CHUNK, m, True)
+        logits(closing[2:], BODY2, BODY1)
+        quantize_h(CHUNK, CHUNK, rounded)
+        scores(0, CHUNK, pairs[-1], True)
+        saturate(3)
+        rounded = rounded_tile(HALF)
+        for c in (2, 3):
+            apply_gain(nc.vector, c, rounded[:, (c - 2) * CHUNK : (c - 1) * CHUNK, :], CHUNK)
+        quantize_h(HALF, HALF, rounded)
+        for m in pairs:
+            scores(CHUNK, CHUNK, m, False)
+        for m in range(S2 // P):
+            scores(HALF, HALF, m, m < 3 or m % 2 == 0)

@@ -51,11 +51,10 @@ def tile_list_sparse_lexical_scores_kernel(
         w4_scales_raw = keep.tile([P, 2, H // 4], I32, align_bytes=64, tag="doc_words")
         gain = keep.tile([P, PACK], F32)
         prior_rows = keep.tile([P, QUAD], F32, align_bytes=64)
-        prior_turned = keep.tile([P, QUAD], F32, align_bytes=64)
-        prior_cols = keep.tile([P, S2 // P], F32)
         body_planes = keep.tile([P, 2, S // 4], I32, align_bytes=64)
         warm = keep.tile([P, 2], F32)
 
+        nc.vector.memset(prior_rows[:], 0.0)
         nc.vector.memset(doc_rows[:], 0)
         nc.vector.memset(text_planes[:], 0)
         nc.vector.memset(warm[:, 0:1], 0.0)
@@ -82,9 +81,7 @@ def tile_list_sparse_lexical_scores_kernel(
         load_text_words(BODY1)
         load_text_words(BODY2)
         nc.scalar.dma_start(w4_raw[:], w4_words.rearrange("a p n -> p a n").bitcast(I32))
-        nc.scalar.dma_start(
-            prior_rows[:], prior.rearrange("(r b) -> r b", b=QUAD).unsqueeze(0).to_broadcast([P // QUAD, QUAD, QUAD])
-        )
+        nc.scalar.dma_start(prior_rows[0:P:PACK, :], prior.rearrange("(m q b) -> q m b", q=P // QUAD, b=QUAD))
         nc.scalar.dma_start(doc_rows[0:P:SPREAD, :], tab2_scales[0].bitcast(I32))
         load_text_scales(nc.scalar, 2)
         load_text_scales(nc.scalar, 3)
@@ -97,10 +94,8 @@ def tile_list_sparse_lexical_scores_kernel(
         def gather_words(codes, table, offsets):
             nc.vector.tensor_copy(codes, table[:].bitcast(U32).indirect(offsets))
 
-        nc.vector.transpose(prior_turned[:], prior_rows[:])
-        for q in range(P // QUAD):
-            quadrant = slice(QUAD * q, QUAD * (q + 1))
-            nc.vector.tensor_copy(prior_cols[quadrant, :], prior_turned[quadrant, q : QUAD : P // QUAD])
+        prior_cols = keep.tile([P, QUAD], F32, align_bytes=64)
+        nc.vector.transpose(prior_cols[:], prior_rows[:])
 
         w4_codes = keep.tile([P, 2, 2 * H], U8, align_bytes=64)
         nc.vector.tensor_copy(
@@ -119,7 +114,7 @@ def tile_list_sparse_lexical_scores_kernel(
         for r in range(PACK):
             nc.sync.dma_start(cand_plane[r:P:QUAD, :], cand_rows[SPREAD * r : P : QUAD, :].bitcast(I32))
 
-        w1_bf = keep.tile([P, PACK * H], BF16, align_bytes=64)
+        w1_bf = keep.tile([P, PACK * H], BF16, align_bytes=64, tag="w1_bf")
         w1_codes = keep.tile([P, H], U32, align_bytes=64)
         w1_plane = keep.tile([P, H], U8, align_bytes=64)
         for tiles in (slice(0, 2), slice(2, 4)):
@@ -139,8 +134,8 @@ def tile_list_sparse_lexical_scores_kernel(
                 gather_words(codes[:, first : first + width], text_words[a], idx[:, entries(half * HALF + first, width)])
 
         gather_queries(TITLE, 0, HALF)
-        w4_planes = keep.tile([P, 2, H], U8, align_bytes=64)
-        nc.vector.tensor_copy(
+        w4_planes = keep.tile([P, 2, H], U8, align_bytes=64, tag="w1_bf")
+        nc.gpsimd.tensor_copy(
             w4_planes[:].rearrange("p a (t m) -> p a t m", t=PACK),
             w4_scales_raw[:].bitcast(U8).rearrange("p a (m t) -> p a t m", t=PACK),
         )
@@ -242,11 +237,11 @@ def tile_list_sparse_lexical_scores_kernel(
                 )
             result = stage.tile([P, tiles, width], F32, name="result")
             if on_vector:
-                priors = prior_cols[:, m : m + tiles].unsqueeze(2).to_broadcast([P, tiles, width])
+                priors = prior_cols[:, PACK * m : PACK * (m + tiles) : PACK].unsqueeze(2).to_broadcast([P, tiles, width])
                 nc.vector.tensor_tensor(result[:], bank[:], priors, ALU.add)
             else:
                 for e in range(tiles):
-                    bias = prior_cols[:, m + e : m + e + 1]
+                    bias = prior_cols[:, PACK * (m + e) : PACK * (m + e) + 1]
                     nc.scalar.activation(result[:, e, :], bank[:, e, :], ACT.Identity, bias=bias)
             rows = out[m * P : (m + tiles) * P, at]
             nc.sync.dma_start(rows.rearrange("(e p) n -> p e n", e=tiles), result[:])

from contextlib import ExitStack

import concourse.mybir as mybir

F32 = mybir.dt.float32
BF16 = mybir.dt.bfloat16
I32 = mybir.dt.int32
U32 = mybir.dt.uint32
U16 = mybir.dt.uint16
U8 = mybir.dt.uint8
FP8X4 = mybir.dt.float8_e4m3fn_x4
FP4X4 = mybir.dt.float4_e2m1fn_x4
ACT = mybir.ActivationFunctionType
ALU = mybir.AluOpType

P = 128
QUAD = 32
PACK = 4
BLOCKS = 16
BANKS = 8
K, H = 1536, 512
T, S = 2048, 1024
T2, S2 = 4096, 1024
TITLE, BODY1, BODY2 = 0, 1, 2
HALF = 512
CHUNK = 256
GROUP = 128
LIST = 16
PLANE_ROWS = 3 * QUAD + PACK
SPREAD = P // BLOCKS
FLOPS = 2 * K * H * S + 2 * H * S2 * S


def tile_list_sparse_lexical_scores_kernel(
    tc, tab_words, tab_scales, tab2_words, tab2_scales, w1, w4_words, w4_scales, g, prior, offs, offs2, out
):
    nc = tc.nc
    with ExitStack() as ctx:
        keep = ctx.enter_context(tc.tile_pool(name="keep", bufs=1))
        stage = ctx.enter_context(tc.tile_pool(name="stage", bufs=S * S2 // (P * HALF)))
        psum = ctx.enter_context(tc.psum_pool(name="psum", bufs=1))

        idx = keep.tile([P, S // LIST], U16)
        idx2 = keep.tile([P, S2 // LIST], U16)
        text_words = [keep.tile([P, T], I32, name=f"words{a}", tag=f"words{a}", align_bytes=64) for a in range(3)]
        w1_raw = keep.tile([P, PACK, H], F32, align_bytes=64)
        text_planes = keep.tile([P, T // 4], I32, align_bytes=64)
        doc_rows = keep.tile([P, T2 // 4], I32, align_bytes=64)
        cand_plane = keep.tile([P, S2 // 4], I32, align_bytes=64)
        w4_raw = keep.tile([P, 2, H // 2], I32, align_bytes=64)
        w4_scales_raw = keep.tile([P, 2, H // 4], I32, align_bytes=64, tag="doc_words")
        gain = keep.tile([P, PACK], F32)
        prior_rows = keep.tile([P, QUAD], F32, align_bytes=64)
        body_planes = keep.tile([P, 2, S // 4], I32, align_bytes=64)
        warm = keep.tile([P, 2], F32)

        nc.vector.memset(prior_rows[:], 0.0)
        nc.vector.memset(doc_rows[:], 0)
        nc.vector.memset(text_planes[:], 0)
        nc.vector.memset(warm[:, 0:1], 0.0)
        nc.vector.memset(w4_scales_raw[:], 0)
        nc.vector.memset(cand_plane[:], 0)
        nc.vector.memset(body_planes[3 * QUAD : P], 0)

        def load_text_words(a):
            nc.sync.dma_start(text_words[a][:], tab_words[a].rearrange("p t i -> p (t i)").bitcast(I32))

        def load_text_scales(queue, q):
            rows = tab_scales[:, PACK * q : PACK * (q + 1), :].bitcast(I32)
            queue.dma_start(text_planes[QUAD * q : QUAD * q + 3 * PACK, :], rows)

        nc.sync.dma_start(idx2[:], offs2)
        nc.sync.dma_start(idx[:], offs)
        nc.sync.dma_start(w1_raw[:], w1.rearrange("(p j) c -> p j c", j=PACK))
        load_text_scales(nc.sync, 0)
        load_text_scales(nc.sync, 1)
        load_text_words(TITLE)
        for r in range(PACK):
            rows = w4_scales[:, r:BLOCKS:PACK, :].rearrange("a q n -> q a n").bitcast(I32)
            nc.sync.dma_start(w4_scales_raw[r:P:QUAD], rows)
        load_text_words(BODY1)
        load_text_words(BODY2)
        nc.scalar.dma_start(w4_raw[:], w4_words.rearrange("a p n -> p a n").bitcast(I32))
        nc.scalar.dma_start(prior_rows[0:P:PACK, :], prior.rearrange("(m q b) -> q m b", q=P // QUAD, b=QUAD))
        nc.scalar.dma_start(doc_rows[0:P:SPREAD, :], tab2_scales[0].bitcast(I32))
        load_text_scales(nc.scalar, 2)
        load_text_scales(nc.scalar, 3)
        nc.scalar.dma_start(gain[:], g.rearrange("(p t) -> p t", t=PACK))
        nc.scalar.activation(warm[:, 1:2], warm[:, 0:1], ACT.Ln, bias=1.0)

        def entries(first, count):
            return slice(first // LIST, (first + count) // LIST)

        def gather_words(codes, table, offsets):
            nc.vector.tensor_copy(codes, table[:].bitcast(U32).indirect(offsets))

        prior_cols = keep.tile([P, QUAD], F32, align_bytes=64)
        nc.vector.transpose(prior_cols[:], prior_rows[:])

        w4_codes = keep.tile([P, 2, 2 * H], U8, align_bytes=64)
        nc.vector.tensor_copy(
            w4_codes[:].bitcast(U16).rearrange("p a (t m) -> p a t m", t=PACK),
            w4_raw[:].bitcast(U16).rearrange("p a (m t) -> p a t m", t=PACK),
        )

        cand_rows = keep.tile([P, S2], U8, align_bytes=64)
        nc.vector.tensor_copy(cand_rows[:], doc_rows[:].bitcast(U8).indirect(idx2[:]))

        query_planes = keep.tile([P, S], U8, align_bytes=64)
        nc.vector.tensor_copy(query_planes[:], text_planes[:].bitcast(U8).indirect(idx[:]))
        for a in (BODY1, BODY2):
            rows = query_planes[PACK * a : PACK * a + PLANE_ROWS, :].bitcast(I32)
            nc.sync.dma_start(body_planes[0:PLANE_ROWS, a - BODY1, :], rows)
        for r in range(PACK):
            nc.sync.dma_start(cand_plane[r:P:QUAD, :], cand_rows[SPREAD * r : P : QUAD, :].bitcast(I32))

        w1_bf = keep.tile([P, PACK * H], BF16, align_bytes=64, tag="w1_bf")
        w1_codes = keep.tile([P, H], U32, align_bytes=64)
        w1_plane = keep.tile([P, H], U8, align_bytes=64)
        for tiles in (slice(0, 2), slice(2, 4)):
            nc.scalar.activation(
                w1_bf[:].rearrange("p (t m j) -> p m j t", t=PACK, j=PACK)[:, :, :, tiles],
                w1_raw[:].rearrange("p j (m t) -> p m j t", t=PACK)[:, :, :, tiles],
                ACT.Identity,
            )
        nc.vector.quantize_mx(out=w1_codes[:].bitcast(FP8X4), scales=w1_plane[:], in_=w1_bf[:])

        query_codes = {}

        def gather_queries(a, half, width):
            codes = keep.tile([P, HALF], U32, name=f"codes{a}{half}", align_bytes=64)
            query_codes[a, half] = codes
            for first in range(0, HALF, width):
                gather_words(codes[:, first : first + width], text_words[a], idx[:, entries(half * HALF + first, width)])

        gather_queries(TITLE, 0, HALF)
        w4_planes = keep.tile([P, 2, H], U8, align_bytes=64, tag="w1_bf")
        nc.gpsimd.tensor_copy(
            w4_planes[:].rearrange("p a (t m) -> p a t m", t=PACK),
            w4_scales_raw[:].bitcast(U8).rearrange("p a (m t) -> p a t m", t=PACK),
        )
        doc_words = keep.tile([P, T2], I32, align_bytes=64, tag="doc_words")
        nc.scalar.dma_start(doc_words[:], tab2_words[0].rearrange("p t i -> p (t i)").bitcast(I32))
        gather_queries(BODY1, 0, HALF)
        gather_queries(BODY2, 0, CHUNK)

        logit_banks = {}

        def logits(steps, first_pass, last_pass):
            for c, a in steps:
                if a == first_pass:
                    logit_banks[c] = psum.tile([P, PACK, GROUP], F32, tag=f"bank{c}", name=f"logit{c}")
                plane = query_planes[:] if a == TITLE else body_planes[:, a - BODY1, :].bitcast(U8)
                half, inside = divmod(c * GROUP, HALF)
                for t in range(PACK):
                    if a == TITLE:
                        weights = w1_codes[:, P * t : P * (t + 1)].bitcast(FP8X4)
                        weight_scales = w1_plane[:, P * t : P * (t + 1)]
                    else:
                        weights = w4_codes[:, a - BODY1, 2 * P * t : 2 * P * (t + 1)].bitcast(FP4X4)
                        weight_scales = w4_planes[:, a - BODY1, P * t : P * (t + 1)]
                    nc.tensor.matmul_mx(
                        out=logit_banks[c][:, t, :],
                        lhsT=weights,
                        lhsT_scale=weight_scales,
                        rhs=query_codes[a, half][:, inside : inside + GROUP].bitcast(FP8X4),
                        rhs_scale=plane[:, c * GROUP : (c + 1) * GROUP],
                        start=(a == first_pass and t == 0),
                        stop=(a == last_pass and t == PACK - 1),
                    )

        groups = range(HALF // GROUP)
        logits([(c, TITLE) for c in groups] + [(c, a) for c in groups for a in (BODY1, BODY2)], TITLE, BODY2)

        gather_queries(BODY2, 1, HALF)
        late_codes = keep.tile([P, 2, HALF], U32, tag=f"words{BODY2}", align_bytes=64)
        for a in (TITLE, BODY1):
            query_codes[a, 1] = late_codes[:, a, :]
            gather_words(late_codes[:, a, :], text_words[a], idx[:, entries(HALF, HALF)])
        groups = range(HALF // GROUP, S // GROUP)
        closing = [(c, BODY1) for c in groups]
        logits([(c, a) for a in (BODY2, TITLE) for c in groups] + closing[:2], BODY2, BODY1)

        h_codes = keep.tile([P, S], U32, align_bytes=64)
        h_plane = keep.tile([P, S], U8, align_bytes=64)
        logs = {}
        cand_codes = {}

        def saturate(c):
            positive = keep.tile([P, CHUNK, PACK], F32, name=f"positive{c}", tag=f"positive{c}", align_bytes=64)
            logs[c] = keep.tile([P, CHUNK, PACK], F32, name=f"logs{c}", align_bytes=64)
            for first in range(0, CHUNK, GROUP):
                bank = logit_banks[(c * CHUNK + first) // GROUP]
                nc.scalar.activation(
                    positive[:, first : first + GROUP, :], bank[:].rearrange("p t n -> p n t"), ACT.Relu
                )
            for first in range(0, CHUNK, GROUP):
                group = slice(first, first + GROUP)
                nc.scalar.activation(logs[c][:, group, :], positive[:, group, :], ACT.Ln, bias=1.0)

        def apply_gain(engine, c, rounded, width):
            gains = gain[:].unsqueeze(1).to_broadcast([P, width, PACK])
            for first in range(0, CHUNK, width):
                part = slice(first, first + width)
                engine.tensor_tensor(rounded[:, part, :], logs[c][:, part, :], gains, ALU.mult)

        def rounded_tile(queries):
            return keep.tile([P, queries, PACK], BF16, name="rounded", tag="rounded", align_bytes=64)

        def quantize_h(first, width, rounded):
            at = slice(first, first + width)
            nc.vector.quantize_mx(
                out=h_codes[:, at].bitcast(FP8X4), scales=h_plane[:, at], in_=rounded[:].rearrange("p n t -> p (n t)")
            )

        def gather_candidates(half, tag):
            cand_codes[half] = keep.tile([P, HALF], U32, name=f"cand_codes{half}", tag=tag, align_bytes=64)
            gather_words(cand_codes[half][:], doc_words, idx2[:, entries(half * HALF, HALF)])

        filled = []

        def scores(first, width, m, on_vector):
            at = slice(first, first + width)
            tiles = HALF // width
            bank = psum.tile([P, tiles, width], F32, tag=f"bank{len(filled) % BANKS}", name=f"score{len(filled)}")
            filled.append(bank)
            for e in range(tiles):
                half, inside = divmod((m + e) * P, HALF)
                nc.tensor.matmul_mx(
                    out=bank[:, e, :],
                    lhsT=cand_codes[half][:, inside : inside + P].bitcast(FP8X4),
                    lhsT_scale=cand_plane[:].bitcast(U8)[:, (m + e) * P : (m + e + 1) * P],
                    rhs=h_codes[:, at].bitcast(FP8X4),
                    rhs_scale=h_plane[:, at],
                    start=True,
                    stop=True,
                )
            result = stage.tile([P, tiles, width], F32, name="result")
            if on_vector:
                priors = prior_cols[:, PACK * m : PACK * (m + tiles) : PACK].unsqueeze(2).to_broadcast([P, tiles, width])
                nc.vector.tensor_tensor(result[:], bank[:], priors, ALU.add)
            else:
                for e in range(tiles):
                    bias = prior_cols[:, PACK * (m + e) : PACK * (m + e) + 1]
                    nc.scalar.activation(result[:, e, :], bank[:, e, :], ACT.Identity, bias=bias)
            rows = out[m * P : (m + tiles) * P, at]
            nc.sync.dma_start(rows.rearrange("(e p) n -> p e n", e=tiles), result[:])

        saturate(0)
        rounded = rounded_tile(CHUNK)
        apply_gain(nc.gpsimd, 0, rounded, GROUP)
        saturate(1)
        gather_candidates(0, "cand_codes0")
        quantize_h(0, CHUNK, rounded)
        gather_candidates(1, "positive1")
        rounded = rounded_tile(CHUNK)
        apply_gain(nc.gpsimd, 1, rounded, CHUNK)
        saturate(2)
        pairs = range(0, S2 // P, HALF // CHUNK)
        for m in pairs[:-1]:
            scores(0, CHUNK, m, True)
        logits(closing[2:], BODY2, BODY1)
        quantize_h(CHUNK, CHUNK, rounded)
        scores(0, CHUNK, pairs[-1], True)
        saturate(3)
        rounded = rounded_tile(HALF)
        for c in (2, 3):
            apply_gain(nc.vector, c, rounded[:, (c - 2) * CHUNK : (c - 1) * CHUNK, :], CHUNK)
        quantize_h(HALF, HALF, rounded)
        for m in pairs:
            scores(CHUNK, CHUNK, m, False)
        for m in range(S2 // P):
            scores(HALF, HALF, m, m < 3 or m % 2 == 0)
